import numpy as np
import ml_dtypes


def mxq(x, axis, fmt="e4m3"):
    dtype, down = {"e4m3": (ml_dtypes.float8_e4m3fn, 7), "e5m2": (ml_dtypes.float8_e5m2, 14)}[fmt]
    v = np.moveaxis(np.asarray(x, np.float32).astype(ml_dtypes.bfloat16).astype(np.float64), axis, -1)
    blocks = v.reshape(v.shape[:-1] + (-1, 32))
    amax = np.abs(blocks).max(-1, keepdims=True)
    byte = np.maximum(np.where(amax > 0, np.frexp(amax)[1] - 1 + 127, 0) - down, 1)
    scale = np.exp2(byte - 127.0)
    codes = (blocks / scale).astype(np.float32).astype(dtype).astype(np.float64)
    return np.moveaxis((codes * scale).reshape(v.shape), -1, axis)


WIDE = False


def mx_kscale(k):
    if not WIDE:
        return np.ones(k)
    levels = np.array([10, -10, 5, -5, 0])
    if k % 512:
        return np.exp2(np.random.permutation(np.resize(levels, k // 32))).repeat(32)
    a = np.empty((k // 512, 16))
    for p in range(k // 512):
        a[p, :8] = np.random.permutation(np.resize(levels, 8))
        for g in range(8):
            far = levels[np.abs(levels - a[p, g]) >= 10]
            a[p, g + 8] = far[np.random.randint(len(far))]
    return np.exp2(a.ravel()).repeat(32)


BF16 = ml_dtypes.bfloat16


def bf(x):
    return np.asarray(x, np.float32).astype(BF16)


def f64(x):
    return np.asarray(x).astype(np.float64)


E2M1 = np.array([0.0, 0.5, 1.0, 1.5, 2.0, 3.0, 4.0, 6.0, -0.0, -0.5, -1.0, -1.5, -2.0, -3.0, -4.0, -6.0])


def pack_weight(w, fmt):
    k, n = w.shape
    w = f64(bf(w)).reshape(k // 32, 32, n)
    amax = np.abs(w).max(1)
    if fmt == "e4m3":
        byte = np.frexp(amax)[1] - 1 + 127 - 7
    else:
        mant, ex = np.frexp(amax / 6.0)
        byte = np.where(mant > 0.5, ex, ex - 1) + 127
    byte = np.clip(np.where(amax > 0, byte, 1), 1, 254)
    scaled = (w * np.exp2(127.0 - byte)[:, None, :]).reshape(k, n).astype(np.float32)
    by_word = np.ascontiguousarray(scaled.reshape(k // 512, 128, 4, n).transpose(0, 1, 3, 2))
    if fmt == "e4m3":
        words = by_word.astype(ml_dtypes.float8_e4m3fn).view(np.uint8)
    else:
        c = by_word.astype(ml_dtypes.float4_e2m1fn).view(np.uint8) & 0xF
        words = c[..., 0::2] | (c[..., 1::2] << 4)
    return np.ascontiguousarray(words), np.ascontiguousarray(byte.astype(np.uint8).reshape(k // 512, 16, n))


def unpack_weight(words, scales, fmt):
    g, p, n, _ = words.shape
    if fmt == "e4m3":
        vals = np.ascontiguousarray(words).view(ml_dtypes.float8_e4m3fn).astype(np.float64)
    else:
        nib = np.empty((g, p, n, 4), np.uint8)
        nib[..., 0::2] = words & 0xF
        nib[..., 1::2] = words >> 4
        vals = E2M1[nib]
    vals = vals * np.repeat(np.exp2(scales.astype(np.float64) - 127.0), 8, axis=1)[..., None]
    return vals.transpose(0, 1, 3, 2).reshape(g * 512, n)

def planes(Y):
    n, m = Y.shape
    b = f64(bf(Y)).reshape(n // 32, 32, m)
    amax = np.abs(b).max(1)
    byte = np.clip(np.where(amax > 0, np.frexp(amax)[1] - 1 + 127 - 7, 1), 1, 254)
    codes = (b * np.exp2(127.0 - byte)[:, None, :]).reshape(n, m).astype(np.float32).astype(ml_dtypes.float8_e4m3fn).view(np.uint8)
    words = codes.reshape(n // 512, 128, 4, m).transpose(0, 1, 3, 2)
    return np.ascontiguousarray(words), np.ascontiguousarray(byte.astype(np.uint8).reshape(n // 512, 16, m))


B, R, W, C, F, N, K3 = 128, 4, 4, 512, 1024, 512, 3
PAD = K3 // 2


def sigmoid(t):
    return 1.0 / (1.0 + np.exp(-t))


def silu(t):
    return t / (1.0 + np.exp(-t))


def depthwise(e, k):
    ep = np.pad(e, ((0, 0), (PAD, PAD), (PAD, PAD), (0, 0)))
    c = np.zeros_like(e)
    for u in range(K3):
        for v in range(K3):
            c = c + k[u, v] * ep[:, u:u + R, v:v + W, :]
    return c


def setup_inputs():
    s = mx_kscale(C)
    g = mx_kscale(C)
    t = mx_kscale(F)
    x = bf(np.random.standard_normal((B, R, W, C)) * s)
    w1_words, w1_scales = pack_weight(np.random.standard_normal((C, F)) / np.sqrt(C) / s[:, None], "e4m3")
    k = bf(0.6 * np.random.standard_normal((K3, K3, F)))
    gs = bf((1.0 + 0.1 * np.random.standard_normal(C)) * g / s)
    ws_words, ws_scales = pack_weight(1.5 * np.sqrt(R * W) * np.random.standard_normal((C, F)) / np.sqrt(C) / g[:, None], "e4m3")
    gp = bf((1.0 + 0.1 * np.random.standard_normal(F)) * t)
    w2_words, w2_scales = pack_weight(3.0 * np.random.standard_normal((F, N)) / np.sqrt(F) / t[:, None], "e4m3")
    return {
        "x": x,
        "w1_words": w1_words,
        "w1_scales": w1_scales,
        "k": k,
        "gs": gs,
        "ws_words": ws_words,
        "ws_scales": ws_scales,
        "gp": gp,
        "w2_words": w2_words,
        "w2_scales": w2_scales,
    }


def core(x, w1_words, w1_scales, k, gs, ws_words, ws_scales, gp, w2_words, w2_scales):
    x = f64(x)
    e = silu(mxq(x.reshape(B * R * W, C), 1, "e4m3") @ unpack_weight(w1_words, w1_scales, "e4m3")).reshape(B, R, W, F)
    c = depthwise(e, f64(k))
    d = silu(c)
    s = np.mean(x, axis=(1, 2)) * f64(gs)
    a = sigmoid(mxq(s, 1, "e4m3") @ unpack_weight(ws_words, ws_scales, "e4m3"))
    p = d * a[:, None, None, :] * f64(gp)
    y = mxq(p.reshape(B * R * W, F), 1, "e4m3") @ unpack_weight(w2_words, w2_scales, "e4m3")
    return y.reshape(B, R, W, N)


def reference(x, w1_words, w1_scales, k, gs, ws_words, ws_scales, gp, w2_words, w2_scales):
    R_out = core(x, w1_words, w1_scales, k, gs, ws_words, ws_scales, gp, w2_words, w2_scales)
    words, scales = planes(np.moveaxis(R_out, 3, 0).reshape(512, -1))
    return R_out, words, scales

@@ -1,0 +1,513 @@
+from contextlib import ExitStack
+
+import concourse.mybir as mybir
+from concourse.masks import make_identity
+
+F32 = mybir.dt.float32
+BF16 = mybir.dt.bfloat16
+I32 = mybir.dt.int32
+U32 = mybir.dt.uint32
+U8 = mybir.dt.uint8
+FP8X4 = mybir.dt.float8_e4m3fn_x4
+ALU = mybir.AluOpType
+ACT = mybir.ActivationFunctionType
+AXIS = mybir.AxisListType
+
+P = 128
+B, POS, C, F, N = 128, 16, 512, 1024, 512
+TOK = B * POS
+FLOPS = 2 * TOK * C * F + 2 * B * C * F + 2 * TOK * F * N + 2 * 9 * TOK * F
+KB = 1024
+X_EVAC = "vsvsvsvs"
+
+
+def tile_mbconvsqueezeexcitelatestage_x2_kernel(
+    tc, x, w1_words, w1_scales, k, gs, ws_words, ws_scales, gp, w2_words, w2_scales, out_0, out_1, out_2
+):
+    nc = tc.nc
+    with ExitStack() as ctx:
+        big = ctx.enter_context(tc.tile_pool(name="big", bufs=1))
+        keep = ctx.enter_context(tc.tile_pool(name="keep", bufs=1))
+        psum = ctx.enter_context(tc.psum_pool(name="psum", bufs=1))
+        ctx.enter_context(tc.manual_schedule())
+
+        def placed(name, shape, dtype, kib, bufs=1):
+            return big.tile(shape, dtype, name=name, tag=name, bufs=bufs, align_bytes=64, offset=kib * KB)
+
+        def kept(name, shape, dtype):
+            return keep.tile(shape, dtype, name=name, tag=name, align_bytes=64)
+
+        def bank(role, shape, dtype=F32):
+            return psum.tile(shape, dtype, name=role, tag=role, bufs={"mm": 3, "tr": 3, "cv": 2}[role])
+
+        ident_f = kept("ident_f", [P, P], F32)
+        ident_b = kept("ident_b", [P, P], BF16)
+        member_f = kept("member_f", [P, 8], F32)
+        member_b = kept("member_b", [P, 8], BF16)
+        warm = kept("warm", [P, 2], F32)
+        k_rows = placed("k_rows", [P, 9, 32], BF16, 108)
+        k_pad = placed("k_pad", [P, 8, 7, 8], BF16, 109)
+        k_part = kept("k_part", [P, 9, 4], BF16)
+        gs_part = kept("gs_part", [P, 4], BF16)
+        gp_part = kept("gp_part", [P, 2, 4], BF16)
+        gp_half = kept("gp_half", [P, 2, 4], F32)
+        raw_planes = placed("raw_planes", [P, 2, F], U8, 106)
+        w2_plane = kept("w2_plane", [P, 2, N], U8)
+        w2_codes = kept("w2_codes", [P, 2, N], U32)
+        w1_codes = kept("w1_codes", [P, F], U32)
+        w1_plane = kept("w1_plane", [P, F], U8)
+        ws_codes = kept("ws_codes", [P, F], U32)
+        ws_plane = kept("ws_plane", [P, F], U8)
+        x_codes = kept("x_codes", [P, TOK], U32)
+        x_plane = kept("x_plane", [P, TOK], U8)
+        s_codes = kept("s_codes", [P, B], U32)
+        s_plane = kept("s_plane", [P, B], U8)
+        p0_codes = kept("p0_codes", [P, TOK], U32)
+        p0_plane = kept("p0_plane", [P, TOK], U8)
+        y_codes = kept("y_codes", [P, TOK], U32)
+        y_plane = kept("y_plane", [P, TOK], U8)
+        gate = kept("gate", [P, 2, B, 4], F32)
+        taps = kept("taps", [P, 6, 16, POS], F32)
+
+        x_raw = [placed("x_raw%d" % c, [P, 4, C], BF16, 128 + 4 * c) for c in range(4)]
+        w1_raw = placed("w1_raw", [P, F], U32, 120)
+        ws_raw = placed("ws_raw", [P, F], U32, 124)
+        windows = placed("windows", [P, POS, 8, 4, 4], BF16, 96)
+        conv_mat = [placed("conv_mat%d" % slot, [P, 2, 16, 8, POS], F32, 64 + 16 * slot) for slot in range(2)]
+        e_vec = placed("e_vec", [P, 2, POS, B], F32, 144)
+        c_vec = placed("c_vec", [P, 2, POS, B], F32, 160)
+
+        x_flat = x.rearrange("b i j c -> (b i j) c")
+        k_flat = k.rearrange("u v f -> (u v) f")
+
+        def load_x(c):
+            nc.sync.dma_start(out=x_raw[c][:], in_=x_flat[512 * c : 512 * (c + 1), :].rearrange("(j p) c -> p j c", p=P))
+
+        def load_words(dst, words):
+            nc.sync.dma_start(out=dst.bitcast(I32), in_=words.rearrange("p n t -> p (n t)").bitcast(I32))
+
+        def load_k_rows(t):
+            nc.gpsimd.dma_start(out=k_rows[32 * t : 32 * (t + 1)], in_=k_flat.rearrange("a (q r) -> q a r", r=32))
+
+        def load_scale_rows(dst, rows):
+            for q in range(4):
+                nc.sync.dma_start(out=dst[32 * q : 32 * q + 4].bitcast(I32), in_=rows[4 * q : 4 * q + 4].bitcast(I32))
+
+        nc.vector.memset(raw_planes[:].rearrange("p a f -> p (a f)").bitcast(I32), 0)
+        nc.vector.memset(warm[:, 0:1], 0.0)
+        nc.vector.memset(k_pad[:].rearrange("p c a b -> p (c a b)").bitcast(I32), 0)
+        nc.vector.memset(w2_plane[:].rearrange("p a f -> p (a f)").bitcast(I32), 0)
+        make_identity(nc, ident_f[:])
+        for t in range(4):
+            load_k_rows(t)
+        make_identity(nc, ident_b[:])
+        nc.scalar.activation(out=warm[:, 1:2], in_=warm[:, 0:1], func=ACT.Silu)
+
+        load_x(0)
+        load_words(w1_raw[:], w1_words[0])
+        load_scale_rows(raw_planes[:, 0, :], w1_scales[0])
+        load_x(1)
+        load_x(2)
+        load_x(3)
+        nc.sync.dma_start(out=k_part[:], in_=k_flat[:, 512:1024].rearrange("a (p t) -> p a t", t=4))
+        nc.sync.dma_start(out=gs_part[:], in_=gs.rearrange("(p t) -> p t", t=4))
+        load_words(ws_raw[:], ws_words[0])
+        load_scale_rows(raw_planes[:, 1, :], ws_scales[0])
+        nc.sync.dma_start(out=gp_part[:], in_=gp.rearrange("(g p t) -> p g t", g=2, t=4))
+        nc.sync.dma_start(
+            out=w2_codes[:].bitcast(I32), in_=w2_words.rearrange("g p n t -> p g (n t)").bitcast(I32)
+        )
+        load_scale_rows(w2_plane[:], w2_scales.rearrange("g r n -> r g n"))
+
+        nc.vector.tensor_reduce(
+            out=member_f[:], in_=ident_f[:].rearrange("p (c s) -> p c s", s=POS), axis=AXIS.X, op=ALU.add
+        )
+        for slot in range(2):
+            nc.vector.memset(conv_mat[slot][:].rearrange("p t r c s -> p (t r c s)"), 0.0)
+        nc.vector.tensor_copy(out=member_b[:], in_=member_f[:])
+
+        def order_w1_tile(tile):
+            g, t = divmod(tile, 4)
+            for src, dst in ((w1_raw[:].bitcast(I32), w1_codes[:].bitcast(I32)), (raw_planes[:, 0, :], w1_plane[:])):
+                if tile < 6:
+                    nc.vector.tensor_copy(
+                        out=dst.rearrange("p (g t a c r) -> p g t a c r", g=2, t=4, a=4, c=8)[:, g, t],
+                        in_=src.rearrange("p (g a r c t) -> p g t a c r", g=2, t=4, a=4, c=8)[:, g, t],
+                    )
+                else:
+                    nc.vector.tensor_copy(
+                        out=dst.rearrange("p (g t m) -> p g t m", g=2, t=4)[:, g, t],
+                        in_=src.rearrange("p (g m t) -> p g t m", g=2, t=4)[:, g, t],
+                    )
+
+        def order_ws():
+            for src, dst in ((ws_raw[:].bitcast(I32), ws_codes[:].bitcast(I32)), (raw_planes[:, 1, :], ws_plane[:])):
+                for g in range(2):
+                    nc.vector.tensor_copy(
+                        out=dst.rearrange("p (g t m) -> p g t m", g=2, t=4)[:, g],
+                        in_=src.rearrange("p (g m t) -> p g t m", g=2, t=4)[:, g],
+                    )
+
+        x_in = {}
+
+        def turn_x(c):
+            x_in[c] = placed("x_in", [P, 512 * 4], BF16, 112, bufs=2)
+            for h in range(2):
+                ps = bank("tr", [P, 2, 2, P])
+                for j in range(2):
+                    words = x_raw[c][:, 2 * h + j, :].bitcast(F32)
+                    for u in range(2):
+                        nc.tensor.transpose(ps[:, j, u, :], words[:, u:256:2], ident_f[:])
+                dst = x_in[c][:].bitcast(F32).rearrange("p (j r u) -> p j r u", j=4, u=2)[:, 2 * h : 2 * h + 2]
+                src = ps[:].rearrange("p j u r -> p j r u")
+                if X_EVAC[2 * c + h] == "v":
+                    nc.vector.tensor_copy(out=dst, in_=src)
+                else:
+                    nc.scalar.copy(out=dst, in_=src)
+
+        def quantize(codes, plane, src):
+            nc.vector.quantize_mx(out=codes.bitcast(FP8X4), scales=plane, in_=src)
+
+        def quantize_x(c):
+            cols = slice(512 * c, 512 * (c + 1))
+            quantize(x_codes[:, cols], x_plane[:, cols], x_in[c][:])
+
+        def mx(out, lhs, lhs_plane, rhs, rhs_plane, start=True, stop=True):
+            nc.tensor.matmul_mx(
+                out=out, lhsT=lhs.bitcast(FP8X4), lhsT_scale=lhs_plane, rhs=rhs.bitcast(FP8X4), rhs_scale=rhs_plane,
+                start=start, stop=stop,
+            )
+
+        e_chan = {}
+
+        def expand(tile, c):
+            ps = bank("mm", [P, 512])
+            ch, cols = slice(P * tile, P * (tile + 1)), slice(512 * c, 512 * (c + 1))
+            mx(ps[:], w1_codes[:, ch], w1_plane[:, ch], x_codes[:, cols], x_plane[:, cols])
+            pair, side = divmod(tile, 2)
+            images = slice(32 * c, 32 * (c + 1))
+            if tile < 6:
+                if pair not in e_chan:
+                    e_chan[pair] = placed("e_chan", [P, POS, 2, B], F32, 0, bufs=2)
+                dst = e_chan[pair][:, :, side, images]
+            else:
+                dst = e_vec[:, side, :, images]
+            nc.scalar.activation(out=dst, in_=ps[:].rearrange("p (b s) -> p s b", s=POS), func=ACT.Silu)
+
+        e_pos = {}
+
+        def regroup(pair):
+            e_pos[pair] = placed("e_pos", [P, 16, 2, B], F32, 32, bufs=2)
+            for grp in range(16):
+                a, r = divmod(grp, 4)
+                nc.sync.dma_start(
+                    out=e_pos[pair][:, grp].rearrange("p t b -> p (t b)"),
+                    in_=e_chan[pair][32 * a + r : 32 * a + 32 : 4].rearrange("p s t b -> p s (t b)"),
+                )
+
+        def build_windows():
+            for t in range(4):
+                rows = slice(32 * t, 32 * (t + 1))
+                nc.scalar.copy(
+                    out=k_pad[rows, :, 2:5, 2:5], in_=k_rows[rows, :, t:32:4].rearrange("p (u v) c -> p c u v", u=3)
+                )
+            for pos in range(POS):
+                i, j = divmod(pos, 4)
+                nc.scalar.copy(out=windows[:, pos], in_=k_pad[:, :, 3 - i : 7 - i, 3 - j : 7 - j])
+
+        def turn_windows(h):
+            ps = bank("tr", [P, 8, P], BF16)
+            for pos in range(8):
+                nc.tensor.transpose(
+                    ps[:, pos, :], windows[:, 8 * h + pos].rearrange("p c i j -> p (c i j)"), ident_b[:]
+                )
+            by_tile = ps[:].rearrange("p s (t g r) -> p g t r s", t=4, g=2)
+            nc.scalar.copy(out=taps[:, 0:4, :, 8 * h : 8 * h + 8], in_=by_tile[:, 0])
+            nc.scalar.copy(out=taps[:, 4:6, :, 8 * h : 8 * h + 8], in_=by_tile[:, 1, 0:2])
+
+        def fill_conv_mat(pair):
+            for ch in range(8):
+                rows = slice(POS * ch, POS * (ch + 1))
+                nc.sync.dma_start(
+                    out=conv_mat[pair % 2][rows, :, :, ch, :].rearrange("p t r s -> p (t r) s"),
+                    in_=taps[rows, 2 * pair : 2 * pair + 2].rearrange("p t r s -> p (t r) s"),
+                )
+
+        s_tiles = {}
+
+        def squeeze_sum():
+            ps = bank("cv", [P, 4, B])
+            for j in range(16):
+                for blk in range(4):
+                    nc.tensor.matmul(
+                        ps[:, blk, 8 * j : 8 * j + 8], lhsT=x_raw[j // 4][:, j % 4, P * blk : P * (blk + 1)],
+                        rhs=member_b[:], start=True, stop=True,
+                    )
+            s_tiles["blk"] = placed("s_blk", [P, 4, B], F32, 112)
+            nc.vector.tensor_copy(out=s_tiles["blk"][:], in_=ps[:])
+
+        def squeeze_rows():
+            ps = bank("tr", [P, 4, P])
+            for blk in range(4):
+                nc.tensor.transpose(ps[:, blk, :], s_tiles["blk"][:, blk, :], ident_f[:])
+            s_tiles["rows"] = placed("s_rows", [P, C], F32, 114)
+            nc.vector.tensor_copy(out=s_tiles["rows"][:], in_=ps[:].rearrange("p a c -> p (a c)"))
+
+        def squeeze_quantize():
+            ps = bank("tr", [P, 4, B])
+            for t in range(4):
+                nc.tensor.transpose(ps[:, t, :], s_tiles["rows"][:, t:C:4], ident_f[:])
+            s_in = placed("s_in", [P, B, 4], BF16, 116)
+            nc.vector.scalar_tensor_tensor(
+                out=s_in[:], in0=ps[:].rearrange("p t b -> p b t"), scalar=1.0 / POS,
+                in1=gs_part[:].unsqueeze(1).to_broadcast([P, B, 4]), op0=ALU.mult, op1=ALU.mult,
+            )
+            nc.vector.tensor_scalar(out=gp_half[:], in0=gp_part[:], scalar1=0.5, scalar2=None, op0=ALU.mult)
+            quantize(s_codes[:], s_plane[:], s_in[:].rearrange("p b t -> p (b t)"))
+
+        def excite(g):
+            ps = bank("mm", [P, 4, B])
+            for t in range(4):
+                ch = slice(512 * g + P * t, 512 * g + P * (t + 1))
+                mx(ps[:, t, :], ws_codes[:, ch], ws_plane[:, ch], s_codes[:], s_plane[:])
+            nc.scalar.activation(out=gate[:, g], in_=ps[:].rearrange("p t b -> p b t"), func=ACT.Tanh, scale=0.5)
+
+        def finish_gate(g):
+            nc.vector.scalar_tensor_tensor(
+                out=gate[:, g], in0=gate[:, g], scalar=1.0,
+                in1=gp_half[:, g].unsqueeze(1).to_broadcast([P, B, 4]), op0=ALU.add, op1=ALU.mult,
+            )
+
+        def vec_tap(side, tap, half):
+            u, v = divmod(tap, 3)
+            weight = k_part[:, tap, 2 + side : 3 + side]
+            acc = c_vec[:, side].rearrange("p (i j) b -> p i (j b)", i=4)
+            src = e_vec[:, side].rearrange("p (i j) b -> p i (j b)", i=4)
+            i0, i1 = max(2 * half, 1 - u), min(2 * half + 2, 5 - u)
+            j0, j1 = max(0, 1 - v), min(4, 5 - v)
+            acc = acc[:, i0:i1, B * j0 : B * j1]
+            src = src[:, i0 + u - 1 : i1 + u - 1, B * (j0 + v - 1) : B * (j1 + v - 1)]
+            if tap == 4:
+                nc.vector.tensor_scalar(out=acc, in0=src, scalar1=weight, scalar2=None, op0=ALU.mult)
+            else:
+                nc.vector.scalar_tensor_tensor(out=acc, in0=src, scalar=weight, in1=acc, op0=ALU.mult, op1=ALU.add)
+
+        def vec_silu(side, half):
+            part = c_vec[:, side, 8 * half : 8 * half + 8, :]
+            nc.scalar.activation(out=part, in_=part, func=ACT.Silu)
+
+        halves = {}
+
+        def vec_gate(quarter):
+            if "t" not in halves:
+                halves["t"] = placed("p1_halves", [P, 2, POS, B, 2], BF16, 144)
+            pos = slice(4 * quarter, 4 * quarter + 4)
+            nc.vector.tensor_tensor(
+                out=halves["t"][:, 1, pos], in0=c_vec[:, :, pos, :].rearrange("p t s b -> p s b t"),
+                in1=gate[:, 1, :, 2:4].unsqueeze(1).to_broadcast([P, 4, B, 2]), op=ALU.mult,
+            )
+
+        d_img = {}
+
+        def convolve(pair, blk, side):
+            if pair not in d_img:
+                d_img[pair] = placed("d_img%d" % pair, [P, 2, POS, P], F32, 96 + 16 * pair)
+            ps = bank("cv", [P, 4, 8, POS])
+            for r in range(4):
+                grp = 4 * blk + r
+                nc.tensor.matmul(
+                    ps[:, r].rearrange("p c s -> p (c s)"), lhsT=e_pos[pair][:, grp, side, :],
+                    rhs=conv_mat[pair % 2][:, side, grp].rearrange("p c s -> p (c s)"), start=True, stop=True,
+                )
+            nc.scalar.activation(
+                out=d_img[pair][:, side, :, 32 * blk : 32 * (blk + 1)],
+                in_=ps[:].rearrange("p r c s -> p s (r c)"), func=ACT.Silu,
+            )
+
+        p_in = {}
+
+        def gate_low(pos):
+            ps = bank("tr", [P, 4, B])
+            for t in range(4):
+                nc.tensor.transpose(ps[:, t, :], d_img[t // 2][:, t % 2, pos, :], ident_f[:])
+            step, s = divmod(pos, 2)
+            if s == 0:
+                p_in[0, step] = placed("p_in", [P, 2, B, 4], BF16, 92, bufs=2)
+            nc.vector.tensor_tensor(
+                out=p_in[0, step][:, s], in0=ps[:].rearrange("p t b -> p b t"), in1=gate[:, 0], op=ALU.mult
+            )
+
+        def quantize_low(step):
+            cols = slice(256 * step, 256 * (step + 1))
+            quantize(p0_codes[:, cols], p0_plane[:, cols], p_in[0, step][:].rearrange("p s b t -> p (s b t)"))
+
+        def gate_high(step):
+            ps = bank("tr", [P, 2, 2, B])
+            for s in range(2):
+                for t in range(2):
+                    nc.tensor.transpose(ps[:, s, t, :], d_img[2][:, t, 2 * step + s, :], ident_f[:])
+            nc.vector.tensor_tensor(
+                out=halves["t"][:, 0, 2 * step : 2 * step + 2], in0=ps[:].rearrange("p s t b -> p s b t"),
+                in1=gate[:, 1, :, 0:2].unsqueeze(1).to_broadcast([P, 2, B, 2]), op=ALU.mult,
+            )
+
+        def join_high(step):
+            p_in[1, step] = placed("p_in", [P, 2, B, 4], BF16, 92, bufs=2)
+            nc.vector.tensor_copy(
+                out=p_in[1, step][:].rearrange("p s b (h t) -> p (s b) h t", h=2),
+                in_=halves["t"][:, :, 2 * step : 2 * step + 2].rearrange("p h s b t -> p (s b) h t"),
+            )
+
+        def quantize_high(step):
+            cols = slice(256 * step, 256 * (step + 1))
+            quantize(x_codes[:, cols], x_plane[:, cols], p_in[1, step][:].rearrange("p s b t -> p (s b t)"))
+
+        y_rows, y_half = {}, {}
+        out_rows = out_0.rearrange("b i j n -> b (i j) n")
+
+        def project(step):
+            y_rows[step] = placed("y_rows", [P, 2, N], F32, 80, bufs=3)
+            for s in range(2):
+                ps = bank("mm", [P, N])
+                tok = slice(256 * step + B * s, 256 * step + B * (s + 1))
+                mx(ps[:], p0_codes[:, tok], p0_plane[:, tok], w2_codes[:, 0], w2_plane[:, 0], True, False)
+                mx(ps[:], x_codes[:, tok], x_plane[:, tok], w2_codes[:, 1], w2_plane[:, 1], False, True)
+                nc.scalar.copy(out=y_rows[step][:, s], in_=ps[:])
+            nc.sync.dma_start(out=out_rows[:, 2 * step : 2 * step + 2, :], in_=y_rows[step][:])
+
+        def round_y(step):
+            y_half[step] = placed("y_half", [P, 2, 2, 256], BF16, 48, bufs=2)
+            for s in range(2):
+                nc.vector.tensor_copy(
+                    out=y_half[step][:, s].rearrange("p u (q e) -> p u q e", e=2),
+                    in_=y_rows[step][:, s].rearrange("p (q u e) -> p u q e", u=2, e=2),
+                )
+
+        y_in = {}
+
+        def turn_y(step):
+            if "t" not in y_in:
+                y_in["t"] = placed("y_in", [P, B, POS, 4], BF16, 0)
+            ps = bank("cv", [P, 2, 2, B])
+            for s in range(2):
+                for u in range(2):
+                    nc.tensor.transpose(ps[:, s, u, :], y_half[step][:, s, u, :].bitcast(F32), ident_f[:])
+            nc.scalar.copy(
+                out=y_in["t"][:].bitcast(F32)[:, :, 2 * step : 2 * step + 2, :], in_=ps[:].rearrange("p s u b -> p b s u")
+            )
+
+        def store_planes():
+            words_out = out_1[0].rearrange("p m t -> p (m t)").bitcast(I32)
+            flat = y_in["t"][:].rearrange("p b s t -> p (b s t)")
+            for c in range(4):
+                cols = slice(512 * c, 512 * (c + 1))
+                quantize(y_codes[:, cols], y_plane[:, cols], flat[:, 2048 * c : 2048 * (c + 1)])
+                nc.sync.dma_start(out=words_out[:, cols], in_=y_codes[:, cols].bitcast(I32))
+            for q in range(4):
+                nc.scalar.dma_start(out=out_2[0, 4 * q : 4 * q + 4].bitcast(I32), in_=y_plane[32 * q : 32 * q + 4].bitcast(I32))
+
+        vec_ops = [(side, tap, half) for side in range(2) for tap in (4, 0, 1, 2, 3, 5, 6, 7, 8) for half in range(2)]
+
+        def vec_taps(a, b):
+            for op in vec_ops[a:b]:
+                vec_tap(*op)
+
+        build_windows()
+        order_w1_tile(0)
+        order_w1_tile(1)
+        turn_x(0)
+        order_w1_tile(6)
+        quantize_x(0)
+        turn_x(1)
+        expand(0, 0)
+        expand(1, 0)
+        order_w1_tile(2)
+        quantize_x(1)
+        turn_x(2)
+        expand(0, 1)
+        expand(1, 1)
+        order_w1_tile(3)
+        quantize_x(2)
+        turn_x(3)
+        expand(0, 2)
+        expand(1, 2)
+        turn_windows(0)
+        turn_windows(1)
+        fill_conv_mat(0)
+        order_w1_tile(7)
+        quantize_x(3)
+        order_w1_tile(4)
+        order_w1_tile(5)
+        order_ws()
+        expand(0, 3)
+        expand(1, 3)
+        regroup(0)
+        fill_conv_mat(1)
+        for c in range(4):
+            expand(6, c)
+        vec_taps(0, 2)
+        expand(2, 0)
+        expand(3, 0)
+        squeeze_sum()
+        vec_taps(2, 4)
+        rounds = [(blk, side) for blk in range(4) for side in range(2)]
+        for n, (blk, side) in enumerate(rounds):
+            convolve(0, blk, side)
+            if n < 3:
+                expand(2, n + 1)
+                expand(3, n + 1)
+            elif n < 7:
+                expand(7, n - 3)
+            if n == 2:
+                regroup(1)
+            if n == 0:
+                squeeze_rows()
+                vec_taps(4, 6)
+            if n == 1:
+                squeeze_quantize()
+                vec_taps(6, 18)
+            if n == 7:
+                excite(0)
+                excite(1)
+        fill_conv_mat(2)
+        vec_taps(18, 20)
+        finish_gate(0)
+        finish_gate(1)
+        vec_taps(20, 36)
+        for n, (blk, side) in enumerate(rounds):
+            if n < 4:
+                expand(4, n)
+                expand(5, n)
+            if n == 3:
+                regroup(2)
+            convolve(1, blk, side)
+            if n in (5, 6):
+                vec_silu(0, n - 5)
+        for n, (blk, side) in enumerate(rounds):
+            convolve(2, blk, side)
+            gate_low(2 * n)
+            gate_low(2 * n + 1)
+            if n > 0:
+                quantize_low(n - 1)
+            if n in (1, 2):
+                vec_silu(1, n - 1)
+            if n in (3, 5):
+                vec_gate(n // 2 - 1)
+        for it in range(8 + 4):
+            if it < 8:
+                gate_high(it)
+            if it == 0:
+                quantize_low(7)
+            if it in (2, 4):
+                vec_gate(it // 2 + 1)
+            if 4 <= it:
+                turn_y(it - 4)
+            if 1 <= it < 9:
+                quantize_high(it - 1)
+            if 3 <= it < 11:
+                round_y(it - 3)
+            if it < 8:
+                join_high(it)
+            if 2 <= it < 10:
+                project(it - 2)
+        store_planes()

@@ -18,7 +18,9 @@ B, POS, C, F, N = 128, 16, 512, 1024, 512
 TOK = B * POS
 FLOPS = 2 * TOK * C * F + 2 * B * C * F + 2 * TOK * F * N + 2 * 9 * TOK * F
 KB = 1024
-X_EVAC = "vsvsvsvs"
+X_EVAC = "vvsvsvsv"
+Y_EVAC = "sssssssv"
+R_ENG = "vvvvvvvvvvvvvvvv"
 
 
 def tile_mbconvsqueezeexcitelatestage_x2_kernel(
@@ -40,18 +42,15 @@ def tile_mbconvsqueezeexcitelatestage_x2_kernel(
         def bank(role, shape, dtype=F32):
             return psum.tile(shape, dtype, name=role, tag=role, bufs={"mm": 3, "tr": 3, "cv": 2}[role])
 
-        ident_f = kept("ident_f", [P, P], F32)
-        ident_b = kept("ident_b", [P, P], BF16)
+        ident = kept("ident", [P, P], F32)
         member_f = kept("member_f", [P, 8], F32)
         member_b = kept("member_b", [P, 8], BF16)
         warm = kept("warm", [P, 2], F32)
-        k_rows = placed("k_rows", [P, 9, 32], BF16, 108)
-        k_pad = placed("k_pad", [P, 8, 7, 8], BF16, 109)
-        k_part = kept("k_part", [P, 9, 4], BF16)
+        k_part = kept("k_part", [P, 9, 8], BF16)
+        k_mid = kept("k_mid", [P, 1], F32)
         gs_part = kept("gs_part", [P, 4], BF16)
-        gp_part = kept("gp_part", [P, 2, 4], BF16)
-        gp_half = kept("gp_half", [P, 2, 4], F32)
-        raw_planes = placed("raw_planes", [P, 2, F], U8, 106)
+        gp_part = kept("gp_part", [P, 8], BF16)
+        gp_half = kept("gp_half", [P, 8], F32)
         w2_plane = kept("w2_plane", [P, 2, N], U8)
         w2_codes = kept("w2_codes", [P, 2, N], U32)
         w1_codes = kept("w1_codes", [P, F], U32)
@@ -66,98 +65,94 @@ def tile_mbconvsqueezeexcitelatestage_x2_kernel(
         p0_plane = kept("p0_plane", [P, TOK], U8)
         y_codes = kept("y_codes", [P, TOK], U32)
         y_plane = kept("y_plane", [P, TOK], U8)
-        gate = kept("gate", [P, 2, B, 4], F32)
-        taps = kept("taps", [P, 6, 16, POS], F32)
+        gate_img = kept("gate_img", [P, 2, P, 4], F32)
+        gate_vec = kept("gate_vec", [P, B, 2], F32)
 
-        x_raw = [placed("x_raw%d" % c, [P, 4, C], BF16, 128 + 4 * c) for c in range(4)]
-        w1_raw = placed("w1_raw", [P, F], U32, 120)
-        ws_raw = placed("ws_raw", [P, F], U32, 124)
-        windows = placed("windows", [P, POS, 8, 4, 4], BF16, 96)
-        conv_mat = [placed("conv_mat%d" % slot, [P, 2, 16, 8, POS], F32, 64 + 16 * slot) for slot in range(2)]
+        x_raw = [placed("x_raw%d" % c, [P, 4, C], BF16, 48 + 4 * c) for c in range(4)]
+        x_tok = [placed("x_tok%d" % h, [P, 8, C], BF16, 96 + 8 * h) for h in range(2)]
+        windows = placed("windows", [P, POS, 6, 4, 4], F32, 112)
+        k_pad = placed("k_pad", [P, 6, 7, 8], F32, 118)
+        w1_raw = placed("w1_raw", [P, F], U32, 128)
+        w1_raw_plane = placed("w1_raw_plane", [P, F], U8, 132)
+        conv_mat = [placed("conv_mat%d" % slot, [P, 16, 8, 2, POS], F32, 64 + 16 * slot) for slot in range(2)]
         e_vec = placed("e_vec", [P, 2, POS, B], F32, 144)
         c_vec = placed("c_vec", [P, 2, POS, B], F32, 160)
 
         x_flat = x.rearrange("b i j c -> (b i j) c")
+        parked = out_0.rearrange("b i j n -> (b i j n)").rearrange("(z p s w) -> z p s w", z=2, p=P, s=POS)
         k_flat = k.rearrange("u v f -> (u v) f")
 
         def load_x(c):
-            nc.sync.dma_start(out=x_raw[c][:], in_=x_flat[512 * c : 512 * (c + 1), :].rearrange("(j p) c -> p j c", p=P))
+            nc.sync.dma_start(out=x_raw[c][:], in_=x[:, c])
+
+        def load_x_tokens(h):
+            nc.sync.dma_start(
+                out=x_tok[h][:], in_=x_flat[1024 * h : 1024 * (h + 1), :].rearrange("(j p) c -> p j c", p=P)
+            )
 
         def load_words(dst, words):
             nc.sync.dma_start(out=dst.bitcast(I32), in_=words.rearrange("p n t -> p (n t)").bitcast(I32))
 
-        def load_k_rows(t):
-            nc.gpsimd.dma_start(out=k_rows[32 * t : 32 * (t + 1)], in_=k_flat.rearrange("a (q r) -> q a r", r=32))
-
-        def load_scale_rows(dst, rows):
+        def load_scale_rows(queue, dst, rows):
             for q in range(4):
-                nc.sync.dma_start(out=dst[32 * q : 32 * q + 4].bitcast(I32), in_=rows[4 * q : 4 * q + 4].bitcast(I32))
+                queue.dma_start(out=dst[32 * q : 32 * q + 4].bitcast(I32), in_=rows[4 * q : 4 * q + 4].bitcast(I32))
 
-        nc.vector.memset(raw_planes[:].rearrange("p a f -> p (a f)").bitcast(I32), 0)
+        nc.vector.memset(w1_raw_plane[:].bitcast(I32), 0)
         nc.vector.memset(warm[:, 0:1], 0.0)
-        nc.vector.memset(k_pad[:].rearrange("p c a b -> p (c a b)").bitcast(I32), 0)
+        nc.vector.memset(k_pad[:].rearrange("p c a b -> p (c a b)"), 0.0)
+        nc.vector.memset(ws_plane[:].bitcast(I32), 0)
         nc.vector.memset(w2_plane[:].rearrange("p a f -> p (a f)").bitcast(I32), 0)
-        make_identity(nc, ident_f[:])
-        for t in range(4):
-            load_k_rows(t)
-        make_identity(nc, ident_b[:])
+        make_identity(nc, ident[:])
         nc.scalar.activation(out=warm[:, 1:2], in_=warm[:, 0:1], func=ACT.Silu)
 
         load_x(0)
+        nc.sync.dma_start(
+            out=k_part[:].rearrange("p a (g t) -> p (a g) t", g=2), in_=k_flat.rearrange("a (g p t) -> p (a g) t", g=2, t=4)
+        )
         load_words(w1_raw[:], w1_words[0])
-        load_scale_rows(raw_planes[:, 0, :], w1_scales[0])
+        load_scale_rows(nc.sync, w1_raw_plane[:], w1_scales[0])
         load_x(1)
         load_x(2)
         load_x(3)
-        nc.sync.dma_start(out=k_part[:], in_=k_flat[:, 512:1024].rearrange("a (p t) -> p a t", t=4))
-        nc.sync.dma_start(out=gs_part[:], in_=gs.rearrange("(p t) -> p t", t=4))
-        load_words(ws_raw[:], ws_words[0])
-        load_scale_rows(raw_planes[:, 1, :], ws_scales[0])
-        nc.sync.dma_start(out=gp_part[:], in_=gp.rearrange("(g p t) -> p g t", g=2, t=4))
-        nc.sync.dma_start(
-            out=w2_codes[:].bitcast(I32), in_=w2_words.rearrange("g p n t -> p g (n t)").bitcast(I32)
+        nc.gpsimd.dma_start(out=gs_part[:], in_=gs.rearrange("(p t) -> p t", t=4))
+        nc.gpsimd.dma_start(
+            out=gp_part[:].rearrange("p (g t) -> p g t", g=2), in_=gp.rearrange("(g p t) -> p g t", g=2, t=4)
         )
-        load_scale_rows(w2_plane[:], w2_scales.rearrange("g r n -> r g n"))
+        load_scale_rows(nc.gpsimd, ws_plane[:], ws_scales[0])
 
         nc.vector.tensor_reduce(
-            out=member_f[:], in_=ident_f[:].rearrange("p (c s) -> p c s", s=POS), axis=AXIS.X, op=ALU.add
+            out=member_f[:], in_=ident[:].rearrange("p (c s) -> p c s", s=POS), axis=AXIS.X, op=ALU.add
         )
         for slot in range(2):
-            nc.vector.memset(conv_mat[slot][:].rearrange("p t r c s -> p (t r c s)"), 0.0)
+            nc.vector.memset(conv_mat[slot][:].rearrange("p r c t s -> p (r c t s)"), 0.0)
         nc.vector.tensor_copy(out=member_b[:], in_=member_f[:])
 
-        def order_w1_tile(tile):
-            g, t = divmod(tile, 4)
-            for src, dst in ((w1_raw[:].bitcast(I32), w1_codes[:].bitcast(I32)), (raw_planes[:, 0, :], w1_plane[:])):
-                if tile < 6:
-                    nc.vector.tensor_copy(
-                        out=dst.rearrange("p (g t a c r) -> p g t a c r", g=2, t=4, a=4, c=8)[:, g, t],
-                        in_=src.rearrange("p (g a r c t) -> p g t a c r", g=2, t=4, a=4, c=8)[:, g, t],
-                    )
-                else:
-                    nc.vector.tensor_copy(
-                        out=dst.rearrange("p (g t m) -> p g t m", g=2, t=4)[:, g, t],
-                        in_=src.rearrange("p (g m t) -> p g t m", g=2, t=4)[:, g, t],
-                    )
+        def load_ws():
+            load_words(ws_codes[:], ws_words[0])
 
-        def order_ws():
-            for src, dst in ((ws_raw[:].bitcast(I32), ws_codes[:].bitcast(I32)), (raw_planes[:, 1, :], ws_plane[:])):
-                for g in range(2):
-                    nc.vector.tensor_copy(
-                        out=dst.rearrange("p (g t m) -> p g t m", g=2, t=4)[:, g],
-                        in_=src.rearrange("p (g m t) -> p g t m", g=2, t=4)[:, g],
-                    )
+        def load_w2():
+            load_scale_rows(nc.sync, w2_plane[:], w2_scales.rearrange("g r n -> r g n"))
+            nc.sync.dma_start(
+                out=w2_codes[:].bitcast(I32), in_=w2_words.rearrange("g p n t -> p g (n t)").bitcast(I32)
+            )
+
+        def order_w1(g, t0, t1):
+            for src, dst in ((w1_raw[:].bitcast(I32), w1_codes[:].bitcast(I32)), (w1_raw_plane[:], w1_plane[:])):
+                nc.vector.tensor_copy(
+                    out=dst.rearrange("p (g t m) -> p g t m", g=2, t=4)[:, g, t0:t1],
+                    in_=src.rearrange("p (g m t) -> p g t m", g=2, t=4)[:, g, t0:t1],
+                )
 
         x_in = {}
 
         def turn_x(c):
-            x_in[c] = placed("x_in", [P, 512 * 4], BF16, 112, bufs=2)
+            x_in[c] = placed("x_in", [P, 512 * 4], BF16, 120, bufs=2)
             for h in range(2):
                 ps = bank("tr", [P, 2, 2, P])
                 for j in range(2):
                     words = x_raw[c][:, 2 * h + j, :].bitcast(F32)
                     for u in range(2):
-                        nc.tensor.transpose(ps[:, j, u, :], words[:, u:256:2], ident_f[:])
+                        nc.tensor.transpose(ps[:, j, u, :], words[:, u:256:2], ident[:])
                 dst = x_in[c][:].bitcast(F32).rearrange("p (j r u) -> p j r u", j=4, u=2)[:, 2 * h : 2 * h + 2]
                 src = ps[:].rearrange("p j u r -> p j r u")
                 if X_EVAC[2 * c + h] == "v":
@@ -185,109 +180,110 @@ def tile_mbconvsqueezeexcitelatestage_x2_kernel(
             ch, cols = slice(P * tile, P * (tile + 1)), slice(512 * c, 512 * (c + 1))
             mx(ps[:], w1_codes[:, ch], w1_plane[:, ch], x_codes[:, cols], x_plane[:, cols])
             pair, side = divmod(tile, 2)
-            images = slice(32 * c, 32 * (c + 1))
             if tile < 6:
-                if pair not in e_chan:
-                    e_chan[pair] = placed("e_chan", [P, POS, 2, B], F32, 0, bufs=2)
-                dst = e_chan[pair][:, :, side, images]
+                if side == 0:
+                    e_chan[pair, c] = placed("e_chan", [P, 4, 2, B], F32, 0, bufs=4)
+                dst = e_chan[pair, c][:, :, side, :]
             else:
-                dst = e_vec[:, side, :, images]
-            nc.scalar.activation(out=dst, in_=ps[:].rearrange("p (b s) -> p s b", s=POS), func=ACT.Silu)
+                dst = e_vec[:, side, 4 * c : 4 * c + 4, :]
+            nc.scalar.activation(out=dst, in_=ps[:].rearrange("p (s b) -> p s b", s=4), func=ACT.Silu)
+            if tile < 6 and side == 1:
+                nc.sync.dma_start(
+                    out=parked[pair % 2, :, 4 * c : 4 * c + 4, :], in_=e_chan[pair, c][:].rearrange("p s t b -> p s (t b)")
+                )
 
         e_pos = {}
 
         def regroup(pair):
-            e_pos[pair] = placed("e_pos", [P, 16, 2, B], F32, 32, bufs=2)
-            for grp in range(16):
-                a, r = divmod(grp, 4)
-                nc.sync.dma_start(
-                    out=e_pos[pair][:, grp].rearrange("p t b -> p (t b)"),
-                    in_=e_chan[pair][32 * a + r : 32 * a + 32 : 4].rearrange("p s t b -> p s (t b)"),
-                )
+            e_pos[pair] = placed("e_pos%d" % pair, [P, 16, 2, B], F32, 16 + 16 * pair)
+            by_group = parked[pair % 2].rearrange("(r c) s w -> (c s) r w", c=8)
+            for blk in range(4):
+                grps = slice(4 * blk, 4 * blk + 4)
+                nc.gpsimd.dma_start(out=e_pos[pair][:, grps].rearrange("p r t b -> p r (t b)"), in_=by_group[:, grps])
 
         def build_windows():
-            for t in range(4):
-                rows = slice(32 * t, 32 * (t + 1))
-                nc.scalar.copy(
-                    out=k_pad[rows, :, 2:5, 2:5], in_=k_rows[rows, :, t:32:4].rearrange("p (u v) c -> p c u v", u=3)
-                )
+            for tap in range(9):
+                u, v = divmod(tap, 3)
+                nc.scalar.copy(out=k_pad[:, :, 4 - u, 4 - v], in_=k_part[:, tap, 0:6])
+            nc.scalar.copy(out=k_mid[:], in_=k_part[:, 4, 7:8])
             for pos in range(POS):
                 i, j = divmod(pos, 4)
                 nc.scalar.copy(out=windows[:, pos], in_=k_pad[:, :, 3 - i : 7 - i, 3 - j : 7 - j])
 
-        def turn_windows(h):
-            ps = bank("tr", [P, 8, P], BF16)
-            for pos in range(8):
-                nc.tensor.transpose(
-                    ps[:, pos, :], windows[:, 8 * h + pos].rearrange("p c i j -> p (c i j)"), ident_b[:]
-                )
-            by_tile = ps[:].rearrange("p s (t g r) -> p g t r s", t=4, g=2)
-            nc.scalar.copy(out=taps[:, 0:4, :, 8 * h : 8 * h + 8], in_=by_tile[:, 0])
-            nc.scalar.copy(out=taps[:, 4:6, :, 8 * h : 8 * h + 8], in_=by_tile[:, 1, 0:2])
+        parked_windows = parked[1].rearrange("p s w -> p (s w)")[:, 0 : POS * 6 * POS].rearrange("p (s w) -> p s w", s=POS)
 
-        def fill_conv_mat(pair):
+        def park_windows(queue, pair0, pair1):
+            cols = slice(32 * pair0, 32 * pair1)
+            queue.dma_start(out=parked_windows[:, :, cols], in_=windows[:].rearrange("p s t i j -> p s (t i j)")[:, :, cols])
+
+        def fill_conv_mat(pair, queue):
+            by_channel = parked_windows.rearrange("(r c) s w -> c s r w", c=8)
             for ch in range(8):
-                rows = slice(POS * ch, POS * (ch + 1))
-                nc.sync.dma_start(
-                    out=conv_mat[pair % 2][rows, :, :, ch, :].rearrange("p t r s -> p (t r) s"),
-                    in_=taps[rows, 2 * pair : 2 * pair + 2].rearrange("p t r s -> p (t r) s"),
+                queue.dma_start(
+                    out=conv_mat[pair % 2][POS * ch : POS * (ch + 1), :, ch].rearrange("p r t s -> p r (t s)"),
+                    in_=by_channel[ch, :, :, 32 * pair : 32 * (pair + 1)],
                 )
 
-        s_tiles = {}
+        s_in = placed("s_in", [P, B, 4], BF16, 133)
 
-        def squeeze_sum():
-            ps = bank("cv", [P, 4, B])
-            for j in range(16):
-                for blk in range(4):
+        sums = {}
+
+        def squeeze(h):
+            if "ps" not in sums:
+                sums["ps"] = bank("cv", [P, 4, B])
+            for j in range(8):
+                images = slice(64 * h + 8 * j, 64 * h + 8 * (j + 1))
+                for t in range(4):
                     nc.tensor.matmul(
-                        ps[:, blk, 8 * j : 8 * j + 8], lhsT=x_raw[j // 4][:, j % 4, P * blk : P * (blk + 1)],
-                        rhs=member_b[:], start=True, stop=True,
+                        sums["ps"][:, t, images], lhsT=x_tok[h][:, j, t:C:4], rhs=member_b[:], start=True, stop=True
                     )
-            s_tiles["blk"] = placed("s_blk", [P, 4, B], F32, 112)
-            nc.vector.tensor_copy(out=s_tiles["blk"][:], in_=ps[:])
 
-        def squeeze_rows():
-            ps = bank("tr", [P, 4, P])
-            for blk in range(4):
-                nc.tensor.transpose(ps[:, blk, :], s_tiles["blk"][:, blk, :], ident_f[:])
-            s_tiles["rows"] = placed("s_rows", [P, C], F32, 114)
-            nc.vector.tensor_copy(out=s_tiles["rows"][:], in_=ps[:].rearrange("p a c -> p (a c)"))
-
-        def squeeze_quantize():
-            ps = bank("tr", [P, 4, B])
-            for t in range(4):
-                nc.tensor.transpose(ps[:, t, :], s_tiles["rows"][:, t:C:4], ident_f[:])
-            s_in = placed("s_in", [P, B, 4], BF16, 116)
+        def scale_s():
+            ps = sums["ps"]
             nc.vector.scalar_tensor_tensor(
                 out=s_in[:], in0=ps[:].rearrange("p t b -> p b t"), scalar=1.0 / POS,
                 in1=gs_part[:].unsqueeze(1).to_broadcast([P, B, 4]), op0=ALU.mult, op1=ALU.mult,
             )
             nc.vector.tensor_scalar(out=gp_half[:], in0=gp_part[:], scalar1=0.5, scalar2=None, op0=ALU.mult)
+
+        def quantize_s():
             quantize(s_codes[:], s_plane[:], s_in[:].rearrange("p b t -> p (b t)"))
 
         def excite(g):
-            ps = bank("mm", [P, 4, B])
-            for t in range(4):
-                ch = slice(512 * g + P * t, 512 * g + P * (t + 1))
-                mx(ps[:, t, :], ws_codes[:, ch], ws_plane[:, ch], s_codes[:], s_plane[:])
-            nc.scalar.activation(out=gate[:, g], in_=ps[:].rearrange("p t b -> p b t"), func=ACT.Tanh, scale=0.5)
+            ps = bank("mm", [P, 512])
+            ch = slice(512 * g, 512 * (g + 1))
+            mx(ps[:], s_codes[:], s_plane[:], ws_codes[:, ch], ws_plane[:, ch])
+            nc.scalar.activation(
+                out=gate_img[:, g].rearrange("p m t -> p (m t)"), in_=ps[:], func=ACT.Tanh, scale=0.5
+            )
 
         def finish_gate(g):
+            ps = bank("tr", [P, 4, P])
+            for t in range(4):
+                nc.tensor.transpose(ps[:, t, :], gp_half[:, 4 * g + t : 4 * g + t + 1].to_broadcast([P, P]), ident[:])
             nc.vector.scalar_tensor_tensor(
-                out=gate[:, g], in0=gate[:, g], scalar=1.0,
-                in1=gp_half[:, g].unsqueeze(1).to_broadcast([P, B, 4]), op0=ALU.add, op1=ALU.mult,
+                out=gate_img[:, g], in0=gate_img[:, g], scalar=1.0,
+                in1=ps[:].rearrange("p t m -> p m t"), op0=ALU.add, op1=ALU.mult,
             )
+
+        def turn_gate():
+            ps = bank("tr", [P, 2, B])
+            for side in range(2):
+                nc.tensor.transpose(ps[:, side, :], gate_img[:, 1, :, 2 + side], ident[:])
+            nc.scalar.copy(out=gate_vec[:], in_=ps[:].rearrange("p t b -> p b t"))
 
         def vec_tap(side, tap, half):
             u, v = divmod(tap, 3)
-            weight = k_part[:, tap, 2 + side : 3 + side]
+            weight = k_part[:, tap, 6 + side : 7 + side]
             acc = c_vec[:, side].rearrange("p (i j) b -> p i (j b)", i=4)
             src = e_vec[:, side].rearrange("p (i j) b -> p i (j b)", i=4)
             i0, i1 = max(2 * half, 1 - u), min(2 * half + 2, 5 - u)
             j0, j1 = max(0, 1 - v), min(4, 5 - v)
             acc = acc[:, i0:i1, B * j0 : B * j1]
             src = src[:, i0 + u - 1 : i1 + u - 1, B * (j0 + v - 1) : B * (j1 + v - 1)]
-            if tap == 4:
+            if tap == 4 and side == 1:
+                nc.scalar.activation(out=acc, in_=src, func=ACT.Copy, scale=k_mid[:])
+            elif tap == 4:
                 nc.vector.tensor_scalar(out=acc, in0=src, scalar1=weight, scalar2=None, op0=ALU.mult)
             else:
                 nc.vector.scalar_tensor_tensor(out=acc, in0=src, scalar=weight, in1=acc, op0=ALU.mult, op1=ALU.add)
@@ -304,55 +300,62 @@ def tile_mbconvsqueezeexcitelatestage_x2_kernel(
             pos = slice(4 * quarter, 4 * quarter + 4)
             nc.vector.tensor_tensor(
                 out=halves["t"][:, 1, pos], in0=c_vec[:, :, pos, :].rearrange("p t s b -> p s b t"),
-                in1=gate[:, 1, :, 2:4].unsqueeze(1).to_broadcast([P, 4, B, 2]), op=ALU.mult,
+                in1=gate_vec[:].unsqueeze(1).to_broadcast([P, 4, B, 2]), op=ALU.mult,
             )
 
-        d_img = {}
+        d_img, p_img, p_in = {}, {}, {}
 
         def convolve(pair, blk, side):
-            if pair not in d_img:
-                d_img[pair] = placed("d_img%d" % pair, [P, 2, POS, P], F32, 96 + 16 * pair)
+            if (pair, blk) not in d_img:
+                d_img[pair, blk] = placed("d_img", [P, 2, POS, 32], F32, 120, bufs=6)
             ps = bank("cv", [P, 4, 8, POS])
             for r in range(4):
                 grp = 4 * blk + r
                 nc.tensor.matmul(
-                    ps[:, r].rearrange("p c s -> p (c s)"), lhsT=e_pos[pair][:, grp, side, :],
-                    rhs=conv_mat[pair % 2][:, side, grp].rearrange("p c s -> p (c s)"), start=True, stop=True,
+                    ps[:, r], lhsT=e_pos[pair][:, grp, side, :], rhs=conv_mat[pair % 2][:, grp, :, side, :],
+                    start=True, stop=True,
                 )
             nc.scalar.activation(
-                out=d_img[pair][:, side, :, 32 * blk : 32 * (blk + 1)],
-                in_=ps[:].rearrange("p r c s -> p s (r c)"), func=ACT.Silu,
+                out=d_img[pair, blk][:, side], in_=ps[:].rearrange("p r c s -> p s (r c)"), func=ACT.Silu,
             )
 
-        p_in = {}
-
-        def gate_low(pos):
-            ps = bank("tr", [P, 4, B])
-            for t in range(4):
-                nc.tensor.transpose(ps[:, t, :], d_img[t // 2][:, t % 2, pos, :], ident_f[:])
-            step, s = divmod(pos, 2)
-            if s == 0:
-                p_in[0, step] = placed("p_in", [P, 2, B, 4], BF16, 92, bufs=2)
+        def gate_block(pair, blk, pos0=0, pos1=POS):
+            if pair not in p_img:
+                p_img[pair] = placed("p_img%d" % pair, [P, POS, P, 2], BF16, 96 + 8 * pair)
+            g, u = divmod(pair, 2)
+            ch = slice(32 * blk, 32 * (blk + 1))
             nc.vector.tensor_tensor(
-                out=p_in[0, step][:, s], in0=ps[:].rearrange("p t b -> p b t"), in1=gate[:, 0], op=ALU.mult
+                out=p_img[pair][:, pos0:pos1, ch, :],
+                in0=d_img[pair, blk][:, :, pos0:pos1, :].rearrange("p t s m -> p s m t"),
+                in1=gate_img[:, g, ch, 2 * u : 2 * u + 2].unsqueeze(1).to_broadcast([P, pos1 - pos0, 32, 2]),
+                op=ALU.mult,
             )
+
+        def p_words(pair, pos):
+            return p_img[pair][:, pos].rearrange("p m t -> p (m t)").bitcast(F32)
+
+        def turn_low(step):
+            ps = bank("tr", [P, 2, 2, B])
+            for s in range(2):
+                for u in range(2):
+                    nc.tensor.transpose(ps[:, s, u, :], p_words(u, 2 * step + s), ident[:])
+            p_in[0, step] = placed("p_in", [P, 2, B, 4], BF16, 36, bufs=4)
+            nc.scalar.copy(out=p_in[0, step][:].bitcast(F32), in_=ps[:].rearrange("p s u b -> p s b u"))
 
         def quantize_low(step):
             cols = slice(256 * step, 256 * (step + 1))
             quantize(p0_codes[:, cols], p0_plane[:, cols], p_in[0, step][:].rearrange("p s b t -> p (s b t)"))
 
-        def gate_high(step):
-            ps = bank("tr", [P, 2, 2, B])
-            for s in range(2):
-                for t in range(2):
-                    nc.tensor.transpose(ps[:, s, t, :], d_img[2][:, t, 2 * step + s, :], ident_f[:])
-            nc.vector.tensor_tensor(
-                out=halves["t"][:, 0, 2 * step : 2 * step + 2], in0=ps[:].rearrange("p s t b -> p s b t"),
-                in1=gate[:, 1, :, 0:2].unsqueeze(1).to_broadcast([P, 2, B, 2]), op=ALU.mult,
+        def turn_high(pos0, pos1):
+            ps = bank("tr", [P, pos1 - pos0, B])
+            for pos in range(pos0, pos1):
+                nc.tensor.transpose(ps[:, pos - pos0, :], p_words(2, pos), ident[:])
+            nc.scalar.copy(
+                out=halves["t"][:, 0, pos0:pos1].rearrange("p s b t -> p s (b t)").bitcast(F32), in_=ps[:]
             )
 
         def join_high(step):
-            p_in[1, step] = placed("p_in", [P, 2, B, 4], BF16, 92, bufs=2)
+            p_in[1, step] = placed("p_in", [P, 2, B, 4], BF16, 36, bufs=4)
             nc.vector.tensor_copy(
                 out=p_in[1, step][:].rearrange("p s b (h t) -> p (s b) h t", h=2),
                 in_=halves["t"][:, :, 2 * step : 2 * step + 2].rearrange("p h s b t -> p (s b) h t"),
@@ -366,7 +369,7 @@ def tile_mbconvsqueezeexcitelatestage_x2_kernel(
         out_rows = out_0.rearrange("b i j n -> b (i j) n")
 
         def project(step):
-            y_rows[step] = placed("y_rows", [P, 2, N], F32, 80, bufs=3)
+            y_rows[step] = placed("y_rows", [P, 2, N], F32, 80, bufs=4)
             for s in range(2):
                 ps = bank("mm", [P, N])
                 tok = slice(256 * step + B * s, 256 * step + B * (s + 1))
@@ -375,13 +378,14 @@ def tile_mbconvsqueezeexcitelatestage_x2_kernel(
                 nc.scalar.copy(out=y_rows[step][:, s], in_=ps[:])
             nc.sync.dma_start(out=out_rows[:, 2 * step : 2 * step + 2, :], in_=y_rows[step][:])
 
-        def round_y(step):
-            y_half[step] = placed("y_half", [P, 2, 2, 256], BF16, 48, bufs=2)
-            for s in range(2):
-                nc.vector.tensor_copy(
-                    out=y_half[step][:, s].rearrange("p u (q e) -> p u q e", e=2),
-                    in_=y_rows[step][:, s].rearrange("p (q u e) -> p u q e", u=2, e=2),
-                )
+        def round_y(step, s):
+            if step not in y_half:
+                y_half[step] = placed("y_half", [P, 2, 2, 256], BF16, 28, bufs=3)
+            engine = nc.gpsimd if R_ENG[2 * step + s] == "g" else nc.vector
+            engine.tensor_copy(
+                out=y_half[step][:, s].rearrange("p u (q e) -> p u q e", e=2),
+                in_=y_rows[step][:, s].rearrange("p (q u e) -> p u q e", u=2, e=2),
+            )
 
         y_in = {}
 
@@ -391,10 +395,13 @@ def tile_mbconvsqueezeexcitelatestage_x2_kernel(
             ps = bank("cv", [P, 2, 2, B])
             for s in range(2):
                 for u in range(2):
-                    nc.tensor.transpose(ps[:, s, u, :], y_half[step][:, s, u, :].bitcast(F32), ident_f[:])
-            nc.scalar.copy(
-                out=y_in["t"][:].bitcast(F32)[:, :, 2 * step : 2 * step + 2, :], in_=ps[:].rearrange("p s u b -> p b s u")
-            )
+                    nc.tensor.transpose(ps[:, s, u, :], y_half[step][:, s, u, :].bitcast(F32), ident[:])
+            dst = y_in["t"][:].bitcast(F32)[:, :, 2 * step : 2 * step + 2, :]
+            src = ps[:].rearrange("p s u b -> p b s u")
+            if Y_EVAC[step] == "v":
+                nc.vector.tensor_copy(out=dst, in_=src)
+            else:
+                nc.scalar.copy(out=dst, in_=src)
 
         def store_planes():
             words_out = out_1[0].rearrange("p m t -> p (m t)").bitcast(I32)
@@ -406,108 +413,221 @@ def tile_mbconvsqueezeexcitelatestage_x2_kernel(
             for q in range(4):
                 nc.scalar.dma_start(out=out_2[0, 4 * q : 4 * q + 4].bitcast(I32), in_=y_plane[32 * q : 32 * q + 4].bitcast(I32))
 
-        vec_ops = [(side, tap, half) for side in range(2) for tap in (4, 0, 1, 2, 3, 5, 6, 7, 8) for half in range(2)]
-
-        def vec_taps(a, b):
-            for op in vec_ops[a:b]:
-                vec_tap(*op)
-
-        build_windows()
-        order_w1_tile(0)
-        order_w1_tile(1)
+        order_w1(0, 2, 4)
         turn_x(0)
-        order_w1_tile(6)
+        order_w1(0, 0, 2)
+        build_windows()
+        park_windows(nc.sync, 0, 2)
         quantize_x(0)
+        load_x_tokens(0)
         turn_x(1)
+        load_x_tokens(1)
+        turn_x(2)
+        quantize_x(2)
+        quantize_x(1)
+        order_w1(1, 2, 4)
         expand(0, 0)
         expand(1, 0)
-        order_w1_tile(2)
-        quantize_x(1)
-        turn_x(2)
-        expand(0, 1)
-        expand(1, 1)
-        order_w1_tile(3)
-        quantize_x(2)
         turn_x(3)
         expand(0, 2)
-        expand(1, 2)
-        turn_windows(0)
-        turn_windows(1)
-        fill_conv_mat(0)
-        order_w1_tile(7)
         quantize_x(3)
-        order_w1_tile(4)
-        order_w1_tile(5)
-        order_ws()
+        expand(1, 2)
+        expand(0, 1)
+        expand(1, 1)
+        fill_conv_mat(1, nc.gpsimd)
         expand(0, 3)
         expand(1, 3)
+        expand(6, 0)
+        order_w1(1, 0, 2)
+        expand(7, 1)
+        expand(6, 3)
+        load_ws()
+        expand(6, 2)
+        expand(6, 1)
+        vec_tap(0, 4, 0)
+        squeeze(0)
+        expand(7, 0)
+        vec_tap(0, 0, 0)
+        vec_tap(0, 4, 1)
+        vec_tap(0, 1, 0)
+        expand(7, 3)
+        expand(7, 2)
+        expand(2, 2)
+        expand(2, 1)
         regroup(0)
-        fill_conv_mat(1)
-        for c in range(4):
-            expand(6, c)
-        vec_taps(0, 2)
+        expand(2, 3)
+        vec_tap(0, 2, 0)
+        vec_tap(0, 3, 0)
+        vec_tap(0, 0, 1)
+        squeeze(1)
+        vec_tap(1, 4, 0)
+        fill_conv_mat(0, nc.sync)
+        expand(3, 2)
+        scale_s()
         expand(2, 0)
+        vec_tap(1, 0, 0)
+        quantize_s()
+        vec_tap(1, 1, 0)
         expand(3, 0)
-        squeeze_sum()
-        vec_taps(2, 4)
-        rounds = [(blk, side) for blk in range(4) for side in range(2)]
-        for n, (blk, side) in enumerate(rounds):
-            convolve(0, blk, side)
-            if n < 3:
-                expand(2, n + 1)
-                expand(3, n + 1)
-            elif n < 7:
-                expand(7, n - 3)
-            if n == 2:
-                regroup(1)
-            if n == 0:
-                squeeze_rows()
-                vec_taps(4, 6)
-            if n == 1:
-                squeeze_quantize()
-                vec_taps(6, 18)
-            if n == 7:
-                excite(0)
-                excite(1)
-        fill_conv_mat(2)
-        vec_taps(18, 20)
+        vec_tap(0, 1, 1)
+        expand(3, 1)
+        vec_tap(1, 4, 1)
+        expand(3, 3)
+        vec_tap(1, 2, 0)
+        vec_tap(0, 5, 0)
+        excite(1)
+        convolve(0, 0, 1)
+        vec_tap(1, 0, 1)
+        excite(0)
+        vec_tap(0, 2, 1)
+        convolve(0, 0, 0)
+        convolve(0, 2, 1)
+        expand(4, 2)
+        regroup(1)
+        expand(5, 2)
+        expand(4, 0)
+        vec_tap(1, 1, 1)
+        vec_tap(1, 3, 0)
+        vec_tap(1, 5, 0)
+        vec_tap(0, 3, 1)
         finish_gate(0)
+        vec_tap(0, 6, 0)
+        vec_tap(1, 6, 0)
+        convolve(0, 2, 0)
+        vec_tap(0, 5, 1)
+        convolve(0, 3, 0)
+        vec_tap(1, 7, 0)
+        expand(4, 1)
+        convolve(0, 1, 0)
+        gate_block(0, 2)
+        vec_tap(1, 8, 0)
+        expand(5, 0)
+        expand(4, 3)
+        convolve(0, 3, 1)
+        expand(5, 3)
+        expand(5, 1)
+        vec_tap(1, 2, 1)
+        convolve(1, 0, 1)
+        convolve(0, 1, 1)
+        vec_tap(0, 7, 0)
+        convolve(1, 2, 0)
+        gate_block(0, 0)
+        regroup(2)
+        convolve(1, 2, 1)
+        vec_tap(0, 8, 0)
         finish_gate(1)
-        vec_taps(20, 36)
-        for n, (blk, side) in enumerate(rounds):
-            if n < 4:
-                expand(4, n)
-                expand(5, n)
-            if n == 3:
-                regroup(2)
-            convolve(1, blk, side)
-            if n in (5, 6):
-                vec_silu(0, n - 5)
-        for n, (blk, side) in enumerate(rounds):
-            convolve(2, blk, side)
-            gate_low(2 * n)
-            gate_low(2 * n + 1)
-            if n > 0:
-                quantize_low(n - 1)
-            if n in (1, 2):
-                vec_silu(1, n - 1)
-            if n in (3, 5):
-                vec_gate(n // 2 - 1)
-        for it in range(8 + 4):
-            if it < 8:
-                gate_high(it)
-            if it == 0:
-                quantize_low(7)
-            if it in (2, 4):
-                vec_gate(it // 2 + 1)
-            if 4 <= it:
-                turn_y(it - 4)
-            if 1 <= it < 9:
-                quantize_high(it - 1)
-            if 3 <= it < 11:
-                round_y(it - 3)
-            if it < 8:
-                join_high(it)
-            if 2 <= it < 10:
-                project(it - 2)
+        convolve(1, 1, 0)
+        convolve(1, 0, 0)
+        convolve(1, 3, 0)
+        gate_block(0, 3)
+        vec_tap(0, 6, 1)
+        park_windows(nc.sync, 2, 3)
+        convolve(1, 3, 1)
+        vec_silu(1, 0)
+        vec_tap(1, 3, 1)
+        gate_block(1, 2)
+        vec_tap(1, 5, 1)
+        vec_tap(1, 6, 1)
+        turn_gate()
+        fill_conv_mat(2, nc.sync)
+        vec_tap(1, 7, 1)
+        vec_tap(1, 8, 1)
+        vec_tap(0, 7, 1)
+        gate_block(0, 1)
+        convolve(1, 1, 1)
+        gate_block(1, 0)
+        convolve(2, 0, 1)
+        gate_block(1, 1)
+        vec_silu(0, 0)
+        convolve(2, 0, 0)
+        convolve(2, 1, 1)
+        gate_block(1, 3)
+        convolve(2, 2, 0)
+        vec_tap(0, 8, 1)
+        convolve(2, 2, 1)
+        gate_block(2, 0)
+        vec_gate(1)
+        turn_low(5)
+        gate_block(2, 2)
+        turn_low(1)
+        vec_silu(0, 1)
+        quantize_low(5)
+        load_w2()
+        convolve(2, 1, 0)
+        convolve(2, 3, 1)
+        turn_low(3)
+        gate_block(2, 1)
+        turn_low(6)
+        quantize_low(1)
+        vec_gate(0)
+        convolve(2, 3, 0)
+        turn_low(0)
+        gate_block(2, 3, 0, 4)
+        quantize_low(3)
+        turn_low(7)
+        gate_block(2, 3, 4, 8)
+        turn_low(2)
+        turn_high(0, 4)
+        turn_high(4, 8)
+        quantize_low(6)
+        gate_block(2, 3, 12, 16)
+        gate_block(2, 3, 8, 12)
+        quantize_low(2)
+        quantize_low(7)
+        join_high(0)
+        quantize_low(0)
+        turn_high(12, 16)
+        quantize_high(0)
+        join_high(3)
+        turn_high(8, 12)
+        vec_silu(1, 1)
+        join_high(2)
+        join_high(1)
+        project(0)
+        quantize_high(2)
+        quantize_high(3)
+        project(2)
+        vec_gate(3)
+        round_y(0, 1)
+        project(3)
+        join_high(6)
+        quantize_high(1)
+        round_y(0, 0)
+        quantize_high(6)
+        project(1)
+        turn_y(0)
+        join_high(7)
+        round_y(2, 0)
+        round_y(2, 1)
+        round_y(3, 0)
+        vec_gate(2)
+        turn_low(4)
+        project(6)
+        round_y(3, 1)
+        turn_y(3)
+        quantize_high(7)
+        project(7)
+        turn_y(2)
+        join_high(5)
+        join_high(4)
+        quantize_high(4)
+        quantize_high(5)
+        round_y(1, 0)
+        project(5)
+        round_y(6, 1)
+        round_y(7, 0)
+        round_y(1, 1)
+        turn_y(1)
+        round_y(7, 1)
+        quantize_low(4)
+        round_y(6, 0)
+        turn_y(7)
+        project(4)
+        turn_y(6)
+        round_y(5, 1)
+        round_y(5, 0)
+        round_y(4, 0)
+        turn_y(5)
+        round_y(4, 1)
+        turn_y(4)
         store_planes()

@@ -19,8 +19,7 @@ TOK = B * POS
 FLOPS = 2 * TOK * C * F + 2 * B * C * F + 2 * TOK * F * N + 2 * 9 * TOK * F
 KB = 1024
 X_EVAC = "vvsvsvsv"
-Y_EVAC = "sssssssv"
-R_ENG = "vvvvvvvvvvvvvvvv"
+Y_EVAC = "svsvsvvv"
 
 
 def tile_mbconvsqueezeexcitelatestage_x2_kernel(
@@ -49,8 +48,6 @@ def tile_mbconvsqueezeexcitelatestage_x2_kernel(
         k_part = kept("k_part", [P, 9, 8], BF16)
         k_mid = kept("k_mid", [P, 1], F32)
         gs_part = kept("gs_part", [P, 4], BF16)
-        gp_part = kept("gp_part", [P, 8], BF16)
-        gp_half = kept("gp_half", [P, 8], F32)
         w2_plane = kept("w2_plane", [P, 2, N], U8)
         w2_codes = kept("w2_codes", [P, 2, N], U32)
         w1_codes = kept("w1_codes", [P, F], U32)
@@ -68,8 +65,8 @@ def tile_mbconvsqueezeexcitelatestage_x2_kernel(
         gate_img = kept("gate_img", [P, 2, P, 4], F32)
         gate_vec = kept("gate_vec", [P, B, 2], F32)
 
-        x_raw = [placed("x_raw%d" % c, [P, 4, C], BF16, 48 + 4 * c) for c in range(4)]
-        x_tok = [placed("x_tok%d" % h, [P, 8, C], BF16, 96 + 8 * h) for h in range(2)]
+        x_raw = [placed("x_raw%d" % c, [P, 4, C], BF16, 96 + 4 * c) for c in range(4)]
+        gp_rows = placed("gp_rows", [P, F], BF16, 136)
         windows = placed("windows", [P, POS, 6, 4, 4], F32, 112)
         k_pad = placed("k_pad", [P, 6, 7, 8], F32, 118)
         w1_raw = placed("w1_raw", [P, F], U32, 128)
@@ -83,12 +80,7 @@ def tile_mbconvsqueezeexcitelatestage_x2_kernel(
         k_flat = k.rearrange("u v f -> (u v) f")
 
         def load_x(c):
-            nc.sync.dma_start(out=x_raw[c][:], in_=x[:, c])
-
-        def load_x_tokens(h):
-            nc.sync.dma_start(
-                out=x_tok[h][:], in_=x_flat[1024 * h : 1024 * (h + 1), :].rearrange("(j p) c -> p j c", p=P)
-            )
+            nc.sync.dma_start(out=x_raw[c][:], in_=x_flat[512 * c : 512 * (c + 1), :].rearrange("(j p) c -> p j c", p=P))
 
         def load_words(dst, words):
             nc.sync.dma_start(out=dst.bitcast(I32), in_=words.rearrange("p n t -> p (n t)").bitcast(I32))
@@ -115,10 +107,8 @@ def tile_mbconvsqueezeexcitelatestage_x2_kernel(
         load_x(2)
         load_x(3)
         nc.gpsimd.dma_start(out=gs_part[:], in_=gs.rearrange("(p t) -> p t", t=4))
-        nc.gpsimd.dma_start(
-            out=gp_part[:].rearrange("p (g t) -> p g t", g=2), in_=gp.rearrange("(g p t) -> p g t", g=2, t=4)
-        )
         load_scale_rows(nc.gpsimd, ws_plane[:], ws_scales[0])
+        nc.gpsimd.dma_start(out=gp_rows[:], in_=gp.partition_broadcast(P))
 
         nc.vector.tensor_reduce(
             out=member_f[:], in_=ident[:].rearrange("p (c s) -> p c s", s=POS), axis=AXIS.X, op=ALU.add
@@ -136,12 +126,19 @@ def tile_mbconvsqueezeexcitelatestage_x2_kernel(
                 out=w2_codes[:].bitcast(I32), in_=w2_words.rearrange("g p n t -> p g (n t)").bitcast(I32)
             )
 
-        def order_w1(g, t0, t1):
+        def order_w1(tile):
+            g, t = divmod(tile, 4)
             for src, dst in ((w1_raw[:].bitcast(I32), w1_codes[:].bitcast(I32)), (w1_raw_plane[:], w1_plane[:])):
-                nc.vector.tensor_copy(
-                    out=dst.rearrange("p (g t m) -> p g t m", g=2, t=4)[:, g, t0:t1],
-                    in_=src.rearrange("p (g m t) -> p g t m", g=2, t=4)[:, g, t0:t1],
-                )
+                if tile < 6:
+                    nc.vector.tensor_copy(
+                        out=dst.rearrange("p (g t a c r) -> p g t a c r", g=2, t=4, a=4, c=8)[:, g, t],
+                        in_=src.rearrange("p (g a r c t) -> p g t a c r", g=2, t=4, a=4, c=8)[:, g, t],
+                    )
+                else:
+                    nc.vector.tensor_copy(
+                        out=dst.rearrange("p (g t m) -> p g t m", g=2, t=4)[:, g, t],
+                        in_=src.rearrange("p (g m t) -> p g t m", g=2, t=4)[:, g, t],
+                    )
 
         x_in = {}
 
@@ -180,26 +177,25 @@ def tile_mbconvsqueezeexcitelatestage_x2_kernel(
             ch, cols = slice(P * tile, P * (tile + 1)), slice(512 * c, 512 * (c + 1))
             mx(ps[:], w1_codes[:, ch], w1_plane[:, ch], x_codes[:, cols], x_plane[:, cols])
             pair, side = divmod(tile, 2)
+            images = slice(32 * c, 32 * (c + 1))
             if tile < 6:
-                if side == 0:
-                    e_chan[pair, c] = placed("e_chan", [P, 4, 2, B], F32, 0, bufs=4)
-                dst = e_chan[pair, c][:, :, side, :]
+                if pair not in e_chan:
+                    e_chan[pair] = placed("e_chan", [P, POS, 2, B], F32, 0, bufs=2)
+                dst = e_chan[pair][:, :, side, images]
             else:
-                dst = e_vec[:, side, 4 * c : 4 * c + 4, :]
-            nc.scalar.activation(out=dst, in_=ps[:].rearrange("p (s b) -> p s b", s=4), func=ACT.Silu)
-            if tile < 6 and side == 1:
-                nc.sync.dma_start(
-                    out=parked[pair % 2, :, 4 * c : 4 * c + 4, :], in_=e_chan[pair, c][:].rearrange("p s t b -> p s (t b)")
-                )
+                dst = e_vec[:, side, :, images]
+            nc.scalar.activation(out=dst, in_=ps[:].rearrange("p (b s) -> p s b", s=POS), func=ACT.Silu)
 
         e_pos = {}
 
-        def regroup(pair):
-            e_pos[pair] = placed("e_pos%d" % pair, [P, 16, 2, B], F32, 16 + 16 * pair)
-            by_group = parked[pair % 2].rearrange("(r c) s w -> (c s) r w", c=8)
-            for blk in range(4):
-                grps = slice(4 * blk, 4 * blk + 4)
-                nc.gpsimd.dma_start(out=e_pos[pair][:, grps].rearrange("p r t b -> p r (t b)"), in_=by_group[:, grps])
+        def regroup(pair, blk):
+            if pair not in e_pos:
+                e_pos[pair] = placed("e_pos", [P, 16, 2, B], F32, 32, bufs=2)
+            for r in range(4):
+                nc.sync.dma_start(
+                    out=e_pos[pair][:, 4 * blk + r].rearrange("p t b -> p (t b)"),
+                    in_=e_chan[pair][32 * blk + r : 32 * blk + 32 : 4].rearrange("p s t b -> p s (t b)"),
+                )
 
         def build_windows():
             for tap in range(9):
@@ -212,9 +208,8 @@ def tile_mbconvsqueezeexcitelatestage_x2_kernel(
 
         parked_windows = parked[1].rearrange("p s w -> p (s w)")[:, 0 : POS * 6 * POS].rearrange("p (s w) -> p s w", s=POS)
 
-        def park_windows(queue, pair0, pair1):
-            cols = slice(32 * pair0, 32 * pair1)
-            queue.dma_start(out=parked_windows[:, :, cols], in_=windows[:].rearrange("p s t i j -> p s (t i j)")[:, :, cols])
+        def park_windows():
+            nc.sync.dma_start(out=parked_windows, in_=windows[:].rearrange("p s t i j -> p s (t i j)"))
 
         def fill_conv_mat(pair, queue):
             by_channel = parked_windows.rearrange("(r c) s w -> c s r w", c=8)
@@ -228,14 +223,14 @@ def tile_mbconvsqueezeexcitelatestage_x2_kernel(
 
         sums = {}
 
-        def squeeze(h):
+        def squeeze(c):
             if "ps" not in sums:
                 sums["ps"] = bank("cv", [P, 4, B])
-            for j in range(8):
-                images = slice(64 * h + 8 * j, 64 * h + 8 * (j + 1))
+            for j in range(4):
+                images = slice(32 * c + 8 * j, 32 * c + 8 * (j + 1))
                 for t in range(4):
                     nc.tensor.matmul(
-                        sums["ps"][:, t, images], lhsT=x_tok[h][:, j, t:C:4], rhs=member_b[:], start=True, stop=True
+                        sums["ps"][:, t, images], lhsT=x_raw[c][:, j, t:C:4], rhs=member_b[:], start=True, stop=True
                     )
 
         def scale_s():
@@ -244,7 +239,6 @@ def tile_mbconvsqueezeexcitelatestage_x2_kernel(
                 out=s_in[:], in0=ps[:].rearrange("p t b -> p b t"), scalar=1.0 / POS,
                 in1=gs_part[:].unsqueeze(1).to_broadcast([P, B, 4]), op0=ALU.mult, op1=ALU.mult,
             )
-            nc.vector.tensor_scalar(out=gp_half[:], in0=gp_part[:], scalar1=0.5, scalar2=None, op0=ALU.mult)
 
         def quantize_s():
             quantize(s_codes[:], s_plane[:], s_in[:].rearrange("p b t -> p (b t)"))
@@ -257,13 +251,13 @@ def tile_mbconvsqueezeexcitelatestage_x2_kernel(
                 out=gate_img[:, g].rearrange("p m t -> p (m t)"), in_=ps[:], func=ACT.Tanh, scale=0.5
             )
 
+        def halve_gp():
+            nc.vector.tensor_scalar(out=gp_rows[:], in0=gp_rows[:], scalar1=0.5, scalar2=None, op0=ALU.mult)
+
         def finish_gate(g):
-            ps = bank("tr", [P, 4, P])
-            for t in range(4):
-                nc.tensor.transpose(ps[:, t, :], gp_half[:, 4 * g + t : 4 * g + t + 1].to_broadcast([P, P]), ident[:])
+            gate = gate_img[:, g].rearrange("p m t -> p (m t)")
             nc.vector.scalar_tensor_tensor(
-                out=gate_img[:, g], in0=gate_img[:, g], scalar=1.0,
-                in1=ps[:].rearrange("p t m -> p m t"), op0=ALU.add, op1=ALU.mult,
+                out=gate, in0=gate, scalar=1.0, in1=gp_rows[:, 512 * g : 512 * (g + 1)], op0=ALU.add, op1=ALU.mult
             )
 
         def turn_gate():
@@ -339,7 +333,7 @@ def tile_mbconvsqueezeexcitelatestage_x2_kernel(
             for s in range(2):
                 for u in range(2):
                     nc.tensor.transpose(ps[:, s, u, :], p_words(u, 2 * step + s), ident[:])
-            p_in[0, step] = placed("p_in", [P, 2, B, 4], BF16, 36, bufs=4)
+            p_in[0, step] = placed("p_in", [P, 2, B, 4], BF16, 54, bufs=4)
             nc.scalar.copy(out=p_in[0, step][:].bitcast(F32), in_=ps[:].rearrange("p s u b -> p s b u"))
 
         def quantize_low(step):
@@ -355,7 +349,7 @@ def tile_mbconvsqueezeexcitelatestage_x2_kernel(
             )
 
         def join_high(step):
-            p_in[1, step] = placed("p_in", [P, 2, B, 4], BF16, 36, bufs=4)
+            p_in[1, step] = placed("p_in", [P, 2, B, 4], BF16, 54, bufs=4)
             nc.vector.tensor_copy(
                 out=p_in[1, step][:].rearrange("p s b (h t) -> p (s b) h t", h=2),
                 in_=halves["t"][:, :, 2 * step : 2 * step + 2].rearrange("p h s b t -> p (s b) h t"),
@@ -368,6 +362,17 @@ def tile_mbconvsqueezeexcitelatestage_x2_kernel(
         y_rows, y_half = {}, {}
         out_rows = out_0.rearrange("b i j n -> b (i j) n")
 
+        def round_y(step, s, src=None):
+            if step not in y_half:
+                y_half[step] = placed("y_half", [P, 2, 2, 256], BF16, 48, bufs=3)
+            src = y_rows[step][:, s] if src is None else src
+            nc.vector.tensor_copy(
+                out=y_half[step][:, s].rearrange("p u (q e) -> p u q e", e=2),
+                in_=src.rearrange("p (q u e) -> p u q e", u=2, e=2),
+            )
+
+        round_inner = round_y
+
         def project(step):
             y_rows[step] = placed("y_rows", [P, 2, N], F32, 80, bufs=4)
             for s in range(2):
@@ -375,17 +380,10 @@ def tile_mbconvsqueezeexcitelatestage_x2_kernel(
                 tok = slice(256 * step + B * s, 256 * step + B * (s + 1))
                 mx(ps[:], p0_codes[:, tok], p0_plane[:, tok], w2_codes[:, 0], w2_plane[:, 0], True, False)
                 mx(ps[:], x_codes[:, tok], x_plane[:, tok], w2_codes[:, 1], w2_plane[:, 1], False, True)
+                if step == 7:
+                    round_inner(step, s, ps[:])
                 nc.scalar.copy(out=y_rows[step][:, s], in_=ps[:])
             nc.sync.dma_start(out=out_rows[:, 2 * step : 2 * step + 2, :], in_=y_rows[step][:])
-
-        def round_y(step, s):
-            if step not in y_half:
-                y_half[step] = placed("y_half", [P, 2, 2, 256], BF16, 28, bufs=3)
-            engine = nc.gpsimd if R_ENG[2 * step + s] == "g" else nc.vector
-            engine.tensor_copy(
-                out=y_half[step][:, s].rearrange("p u (q e) -> p u q e", e=2),
-                in_=y_rows[step][:, s].rearrange("p (q u e) -> p u q e", u=2, e=2),
-            )
 
         y_in = {}
 
@@ -413,221 +411,115 @@ def tile_mbconvsqueezeexcitelatestage_x2_kernel(
             for q in range(4):
                 nc.scalar.dma_start(out=out_2[0, 4 * q : 4 * q + 4].bitcast(I32), in_=y_plane[32 * q : 32 * q + 4].bitcast(I32))
 
-        order_w1(0, 2, 4)
-        turn_x(0)
-        order_w1(0, 0, 2)
+        tap_order = (4, 0, 1, 2, 3, 5, 6, 7, 8)
+        taps_left = [(side, tap, half) for side in range(2) for tap in tap_order for half in range(2)]
+        taps_left = [op for op in taps_left if op[:2] != (1, 4)]
+
+        def run_taps(count):
+            for op in taps_left[:count]:
+                vec_tap(*op)
+                taps_left.remove(op)
+
         build_windows()
-        park_windows(nc.sync, 0, 2)
-        quantize_x(0)
-        load_x_tokens(0)
-        turn_x(1)
-        load_x_tokens(1)
-        turn_x(2)
-        quantize_x(2)
-        quantize_x(1)
-        order_w1(1, 2, 4)
-        expand(0, 0)
-        expand(1, 0)
-        turn_x(3)
-        expand(0, 2)
-        quantize_x(3)
-        expand(1, 2)
-        expand(0, 1)
-        expand(1, 1)
-        fill_conv_mat(1, nc.gpsimd)
-        expand(0, 3)
-        expand(1, 3)
-        expand(6, 0)
-        order_w1(1, 0, 2)
-        expand(7, 1)
-        expand(6, 3)
         load_ws()
-        expand(6, 2)
-        expand(6, 1)
-        vec_tap(0, 4, 0)
-        squeeze(0)
-        expand(7, 0)
-        vec_tap(0, 0, 0)
-        vec_tap(0, 4, 1)
-        vec_tap(0, 1, 0)
-        expand(7, 3)
-        expand(7, 2)
-        expand(2, 2)
-        expand(2, 1)
-        regroup(0)
-        expand(2, 3)
-        vec_tap(0, 2, 0)
-        vec_tap(0, 3, 0)
-        vec_tap(0, 0, 1)
-        squeeze(1)
-        vec_tap(1, 4, 0)
+        park_windows()
         fill_conv_mat(0, nc.sync)
-        expand(3, 2)
+        fill_conv_mat(1, nc.gpsimd)
+        order_w1(0)
+        order_w1(1)
+        turn_x(0)
+        quantize_x(0)
+        turn_x(1)
+        for c in range(4):
+            if c < 3:
+                quantize_x(c + 1)
+            if c < 2:
+                turn_x(c + 2)
+            expand(0, c)
+            expand(1, c)
+            squeeze(c)
+            order_w1((6, 2, 3, 7)[c])
+        for blk in range(4):
+            regroup(0, blk)
         scale_s()
-        expand(2, 0)
-        vec_tap(1, 0, 0)
+        halve_gp()
         quantize_s()
-        vec_tap(1, 1, 0)
-        expand(3, 0)
-        vec_tap(0, 1, 1)
-        expand(3, 1)
-        vec_tap(1, 4, 1)
-        expand(3, 3)
-        vec_tap(1, 2, 0)
-        vec_tap(0, 5, 0)
-        excite(1)
-        convolve(0, 0, 1)
-        vec_tap(1, 0, 1)
+        order_w1(4)
+        order_w1(5)
+        tile_order = ((6,), (7,), (2, 3), (4, 5))
+        expands_left = [(tile, c) for group in tile_order for c in range(4) for tile in group]
+
+        def run_expands(count):
+            for tile, c in expands_left[:count]:
+                expand(tile, c)
+                expands_left.remove((tile, c))
+                if (tile, c) == (3, 3):
+                    for blk in range(4):
+                        regroup(1, blk)
+                if (tile, c) == (7, 3):
+                    vec_tap(1, 4, 0)
+                    vec_tap(1, 4, 1)
+
+        run_expands(6)
         excite(0)
-        vec_tap(0, 2, 1)
-        convolve(0, 0, 0)
-        convolve(0, 2, 1)
-        expand(4, 2)
-        regroup(1)
-        expand(5, 2)
-        expand(4, 0)
-        vec_tap(1, 1, 1)
-        vec_tap(1, 3, 0)
-        vec_tap(1, 5, 0)
-        vec_tap(0, 3, 1)
+        excite(1)
+        run_taps(4)
         finish_gate(0)
-        vec_tap(0, 6, 0)
-        vec_tap(1, 6, 0)
-        convolve(0, 2, 0)
-        vec_tap(0, 5, 1)
-        convolve(0, 3, 0)
-        vec_tap(1, 7, 0)
-        expand(4, 1)
-        convolve(0, 1, 0)
-        gate_block(0, 2)
-        vec_tap(1, 8, 0)
-        expand(5, 0)
-        expand(4, 3)
-        convolve(0, 3, 1)
-        expand(5, 3)
-        expand(5, 1)
-        vec_tap(1, 2, 1)
-        convolve(1, 0, 1)
-        convolve(0, 1, 1)
-        vec_tap(0, 7, 0)
-        convolve(1, 2, 0)
-        gate_block(0, 0)
-        regroup(2)
-        convolve(1, 2, 1)
-        vec_tap(0, 8, 0)
         finish_gate(1)
-        convolve(1, 1, 0)
-        convolve(1, 0, 0)
-        convolve(1, 3, 0)
-        gate_block(0, 3)
-        vec_tap(0, 6, 1)
-        park_windows(nc.sync, 2, 3)
-        convolve(1, 3, 1)
-        vec_silu(1, 0)
-        vec_tap(1, 3, 1)
-        gate_block(1, 2)
-        vec_tap(1, 5, 1)
-        vec_tap(1, 6, 1)
-        turn_gate()
-        fill_conv_mat(2, nc.sync)
-        vec_tap(1, 7, 1)
-        vec_tap(1, 8, 1)
-        vec_tap(0, 7, 1)
-        gate_block(0, 1)
-        convolve(1, 1, 1)
-        gate_block(1, 0)
-        convolve(2, 0, 1)
-        gate_block(1, 1)
-        vec_silu(0, 0)
-        convolve(2, 0, 0)
-        convolve(2, 1, 1)
-        gate_block(1, 3)
-        convolve(2, 2, 0)
-        vec_tap(0, 8, 1)
-        convolve(2, 2, 1)
-        gate_block(2, 0)
-        vec_gate(1)
-        turn_low(5)
-        gate_block(2, 2)
-        turn_low(1)
-        vec_silu(0, 1)
-        quantize_low(5)
-        load_w2()
-        convolve(2, 1, 0)
-        convolve(2, 3, 1)
-        turn_low(3)
-        gate_block(2, 1)
-        turn_low(6)
-        quantize_low(1)
-        vec_gate(0)
-        convolve(2, 3, 0)
-        turn_low(0)
-        gate_block(2, 3, 0, 4)
-        quantize_low(3)
-        turn_low(7)
-        gate_block(2, 3, 4, 8)
-        turn_low(2)
-        turn_high(0, 4)
-        turn_high(4, 8)
-        quantize_low(6)
-        gate_block(2, 3, 12, 16)
-        gate_block(2, 3, 8, 12)
-        quantize_low(2)
-        quantize_low(7)
-        join_high(0)
-        quantize_low(0)
-        turn_high(12, 16)
-        quantize_high(0)
-        join_high(3)
-        turn_high(8, 12)
-        vec_silu(1, 1)
-        join_high(2)
-        join_high(1)
-        project(0)
-        quantize_high(2)
-        quantize_high(3)
-        project(2)
-        vec_gate(3)
-        round_y(0, 1)
-        project(3)
-        join_high(6)
-        quantize_high(1)
-        round_y(0, 0)
-        quantize_high(6)
-        project(1)
-        turn_y(0)
-        join_high(7)
-        round_y(2, 0)
-        round_y(2, 1)
-        round_y(3, 0)
-        vec_gate(2)
-        turn_low(4)
-        project(6)
-        round_y(3, 1)
-        turn_y(3)
-        quantize_high(7)
-        project(7)
-        turn_y(2)
-        join_high(5)
-        join_high(4)
-        quantize_high(4)
-        quantize_high(5)
-        round_y(1, 0)
-        project(5)
-        round_y(6, 1)
-        round_y(7, 0)
-        round_y(1, 1)
-        turn_y(1)
-        round_y(7, 1)
-        quantize_low(4)
-        round_y(6, 0)
-        turn_y(7)
-        project(4)
-        turn_y(6)
-        round_y(5, 1)
-        round_y(5, 0)
-        round_y(4, 0)
-        turn_y(5)
-        round_y(4, 1)
-        turn_y(4)
+        run_expands(2)
+        run_taps(8)
+        rounds = [(pair, blk, side) for pair in range(3) for blk in range(4) for side in range(2)]
+        for n, (pair, blk, side) in enumerate(rounds):
+            convolve(pair, blk, side)
+            run_expands(2)
+            if n == 0:
+                turn_gate()
+            if n == 7:
+                fill_conv_mat(2, nc.gpsimd)
+            if n == 12:
+                for late in range(4):
+                    regroup(2, late)
+                load_w2()
+            if side == 1 and n < 23:
+                gate_block(pair, blk)
+                run_taps(3)
+            if n in (11, 11 + 1):
+                vec_silu(0, n - 11)
+            if n in (16, 16 + 1):
+                vec_silu(1, n - 16)
+            if n >= 17 and side == 1:
+                first = 2 * ((n - 17) // 2)
+                for step in range(first, min(first + 2, 8)):
+                    turn_low(step)
+            if n >= 17 + 2 and side == 1:
+                first = 2 * ((n - 17) // 2 - 1)
+                for step in range(first, min(first + 2, 8)):
+                    quantize_low(step)
+            if n >= 16 and side == 0 and (n - 16) // 2 < 4:
+                vec_gate((n - 16) // 2)
+        for quarter in range(4):
+            gate_block(2, 3, 4 * quarter, 4 * quarter + 4)
+        done_low = min(8, 2 * ((23 - 17) // 2 + 1))
+        done_q = min(8, 2 * ((23 - 17) // 2))
+        for step in range(done_low, 8):
+            turn_low(step)
+        done_gate = min(4, (22 - 16) // 2 + 1)
+        for it in range(8 + 5):
+            if it < 4:
+                turn_high(4 * it, 4 * it + 4)
+            if 5 <= it:
+                turn_y(it - 5)
+            if done_gate + it < 4:
+                vec_gate(done_gate + it)
+            if it < 8:
+                join_high(it)
+            if done_q + it < 8:
+                quantize_low(done_q + it)
+            if 3 <= it < 7 + 3:
+                round_y(it - 3, 0)
+                round_y(it - 3, 1)
+            if it < 8:
+                quantize_high(it)
+            if 2 <= it < 8 + 2:
+                project(it - 2)
         store_planes()

@@ -180,7 +180,7 @@ def tile_mbconvsqueezeexcitelatestage_x2_kernel(
             images = slice(32 * c, 32 * (c + 1))
             if tile < 6:
                 if pair not in e_chan:
-                    e_chan[pair] = placed("e_chan", [P, POS, 2, B], F32, 0, bufs=2)
+                    e_chan[pair] = placed("e_chan%d" % pair, [P, POS, 2, B], F32, 16 * (pair % 2))
                 dst = e_chan[pair][:, :, side, images]
             else:
                 dst = e_vec[:, side, :, images]
@@ -190,9 +190,10 @@ def tile_mbconvsqueezeexcitelatestage_x2_kernel(
 
         def regroup(pair, blk):
             if pair not in e_pos:
-                e_pos[pair] = placed("e_pos", [P, 16, 2, B], F32, 32, bufs=2)
+                e_pos[pair] = placed("e_pos%d" % pair, [P, 16, 2, B], F32, 32 + 16 * (pair % 2))
             for r in range(4):
-                nc.sync.dma_start(
+                queue = nc.sync if blk == 0 or r == 0 else nc.gpsimd
+                queue.dma_start(
                     out=e_pos[pair][:, 4 * blk + r].rearrange("p t b -> p (t b)"),
                     in_=e_chan[pair][32 * blk + r : 32 * blk + 32 : 4].rearrange("p s t b -> p s (t b)"),
                 )
@@ -299,18 +300,20 @@ def tile_mbconvsqueezeexcitelatestage_x2_kernel(
 
         d_img, p_img, p_in = {}, {}, {}
 
-        def convolve(pair, blk, side):
+        def convolve(pair, blk, half):
             if (pair, blk) not in d_img:
                 d_img[pair, blk] = placed("d_img", [P, 2, POS, 32], F32, 120, bufs=6)
-            ps = bank("cv", [P, 4, 8, POS])
-            for r in range(4):
-                grp = 4 * blk + r
-                nc.tensor.matmul(
-                    ps[:, r], lhsT=e_pos[pair][:, grp, side, :], rhs=conv_mat[pair % 2][:, grp, :, side, :],
-                    start=True, stop=True,
-                )
+            ps = bank("cv", [P, 2, 2, 8, POS])
+            for r in range(2):
+                grp = 4 * blk + 2 * half + r
+                for side in range(2):
+                    nc.tensor.matmul(
+                        ps[:, side, r], lhsT=e_pos[pair][:, grp, side, :], rhs=conv_mat[pair % 2][:, grp, :, side, :],
+                        start=True, stop=True,
+                    )
             nc.scalar.activation(
-                out=d_img[pair, blk][:, side], in_=ps[:].rearrange("p r c s -> p s (r c)"), func=ACT.Silu,
+                out=d_img[pair, blk][:, :, :, 16 * half : 16 * (half + 1)],
+                in_=ps[:].rearrange("p t r c s -> p t s (r c)"), func=ACT.Silu,
             )
 
         def gate_block(pair, blk, pos0=0, pos1=POS):
@@ -416,7 +419,7 @@ def tile_mbconvsqueezeexcitelatestage_x2_kernel(
         taps_left = [op for op in taps_left if op[:2] != (1, 4)]
 
         def run_taps(count):
-            for op in taps_left[:count]:
+            for op in [op for op in taps_left if (6 + op[0], 3) not in expands_left][:count]:
                 vec_tap(*op)
                 taps_left.remove(op)
 
@@ -437,15 +440,14 @@ def tile_mbconvsqueezeexcitelatestage_x2_kernel(
                 turn_x(c + 2)
             expand(0, c)
             expand(1, c)
-            squeeze(c)
+            if c < 3:
+                squeeze(c)
             order_w1((6, 2, 3, 7)[c])
         for blk in range(4):
             regroup(0, blk)
-        scale_s()
-        halve_gp()
-        quantize_s()
         order_w1(4)
         order_w1(5)
+        halve_gp()
         tile_order = ((6,), (7,), (2, 3), (4, 5))
         expands_left = [(tile, c) for group in tile_order for c in range(4) for tile in group]
 
@@ -460,31 +462,49 @@ def tile_mbconvsqueezeexcitelatestage_x2_kernel(
                     vec_tap(1, 4, 0)
                     vec_tap(1, 4, 1)
 
+        for c in range(3, 4):
+            run_expands(1)
+            squeeze(c)
+        run_taps(1)
+        scale_s()
+        run_taps(0)
+        quantize_s()
         run_expands(6)
-        excite(0)
-        excite(1)
+        if -1 < 0:
+            excite(0)
+            excite(1)
         run_taps(4)
-        finish_gate(0)
-        finish_gate(1)
-        run_expands(2)
+        if -1 < 0:
+            finish_gate(0)
+            finish_gate(1)
+        run_expands(0)
         run_taps(8)
+        blocks_left = [(pair, blk) for pair in range(3) for blk in range(4)][:11]
         rounds = [(pair, blk, side) for pair in range(3) for blk in range(4) for side in range(2)]
         for n, (pair, blk, side) in enumerate(rounds):
             convolve(pair, blk, side)
             run_expands(2)
-            if n == 0:
+            if n == -1:
+                excite(0)
+                excite(1)
+                finish_gate(0)
+                finish_gate(1)
+            if n == 1:
                 turn_gate()
             if n == 7:
-                fill_conv_mat(2, nc.gpsimd)
-            if n == 12:
+                fill_conv_mat(2, nc.sync)
+            if n == 8:
                 for late in range(4):
                     regroup(2, late)
                 load_w2()
-            if side == 1 and n < 23:
-                gate_block(pair, blk)
+            if side == 1:
+                for done in blocks_left[: 1 if n < 10 else 2]:
+                    if 8 * done[0] + 2 * done[1] + 2 * (1 if n < 10 else 0) < n:
+                        gate_block(*done)
+                        blocks_left.remove(done)
                 run_taps(3)
-            if n in (11, 11 + 1):
-                vec_silu(0, n - 11)
+            if n in (13, 13 + 1):
+                vec_silu(0, n - 13)
             if n in (16, 16 + 1):
                 vec_silu(1, n - 16)
             if n >= 17 and side == 1:
@@ -507,8 +527,10 @@ def tile_mbconvsqueezeexcitelatestage_x2_kernel(
         for it in range(8 + 5):
             if it < 4:
                 turn_high(4 * it, 4 * it + 4)
-            if 5 <= it:
-                turn_y(it - 5)
+            if it % 1 == 0:
+                for step in range(it - 5, it - 5 + 1):
+                    if 0 <= step < 8:
+                        turn_y(step)
             if done_gate + it < 4:
                 vec_gate(done_gate + it)
             if it < 8:

@@ -17,9 +17,15 @@ P = 128
 B, POS, C, F, N = 128, 16, 512, 1024, 512
 TOK = B * POS
 FLOPS = 2 * TOK * C * F + 2 * B * C * F + 2 * TOK * F * N + 2 * 9 * TOK * F
-KB = 1024
-X_EVAC = "vvsvsvsv"
-Y_EVAC = "svsvsvvv"
+KIB = 1024
+
+CHUNKS = 4
+PE_TILES = 6
+STEPS = 8
+CENTRE = 4
+BANKS = {"mm": 3, "tr": 3, "cv": 2}
+X_BANKS_ON_SCALAR = (2, 4, 6)
+Y_STEPS_ON_SCALAR = (0, 2, 4)
 
 
 def tile_mbconvsqueezeexcitelatestage_x2_kernel(
@@ -33,13 +39,13 @@ def tile_mbconvsqueezeexcitelatestage_x2_kernel(
         ctx.enter_context(tc.manual_schedule())
 
         def placed(name, shape, dtype, kib, bufs=1):
-            return big.tile(shape, dtype, name=name, tag=name, bufs=bufs, align_bytes=64, offset=kib * KB)
+            return big.tile(shape, dtype, name=name, tag=name, bufs=bufs, align_bytes=64, offset=kib * KIB)
 
         def kept(name, shape, dtype):
             return keep.tile(shape, dtype, name=name, tag=name, align_bytes=64)
 
-        def bank(role, shape, dtype=F32):
-            return psum.tile(shape, dtype, name=role, tag=role, bufs={"mm": 3, "tr": 3, "cv": 2}[role])
+        def bank(role, shape):
+            return psum.tile(shape, F32, name=role, tag=role, bufs=BANKS[role])
 
         ident = kept("ident", [P, P], F32)
         member_f = kept("member_f", [P, 8], F32)
@@ -60,27 +66,34 @@ def tile_mbconvsqueezeexcitelatestage_x2_kernel(
         s_plane = kept("s_plane", [P, B], U8)
         p0_codes = kept("p0_codes", [P, TOK], U32)
         p0_plane = kept("p0_plane", [P, TOK], U8)
+        p1_codes, p1_plane = x_codes, x_plane
         y_codes = kept("y_codes", [P, TOK], U32)
         y_plane = kept("y_plane", [P, TOK], U8)
         gate_img = kept("gate_img", [P, 2, P, 4], F32)
         gate_vec = kept("gate_vec", [P, B, 2], F32)
 
-        x_raw = [placed("x_raw%d" % c, [P, 4, C], BF16, 96 + 4 * c) for c in range(4)]
+        x_raw = [placed("x_raw%d" % c, [P, 4, C], BF16, 96 + 4 * c) for c in range(CHUNKS)]
         gp_rows = placed("gp_rows", [P, F], BF16, 136)
-        windows = placed("windows", [P, POS, 6, 4, 4], F32, 112)
-        k_pad = placed("k_pad", [P, 6, 7, 8], F32, 118)
+        windows = placed("windows", [P, POS, PE_TILES, 4, 4], F32, 112)
+        k_pad = placed("k_pad", [P, PE_TILES, 7, 8], F32, 118)
         w1_raw = placed("w1_raw", [P, F], U32, 128)
         w1_raw_plane = placed("w1_raw_plane", [P, F], U8, 132)
         conv_mat = [placed("conv_mat%d" % slot, [P, 16, 8, 2, POS], F32, 64 + 16 * slot) for slot in range(2)]
         e_vec = placed("e_vec", [P, 2, POS, B], F32, 144)
         c_vec = placed("c_vec", [P, 2, POS, B], F32, 160)
+        s_in = placed("s_in", [P, B, 4], BF16, 133)
 
         x_flat = x.rearrange("b i j c -> (b i j) c")
-        parked = out_0.rearrange("b i j n -> (b i j n)").rearrange("(z p s w) -> z p s w", z=2, p=P, s=POS)
         k_flat = k.rearrange("u v f -> (u v) f")
+        out_rows = out_0.rearrange("b i j n -> b (i j) n")
+        parked = out_0.rearrange("b i j n -> (b i j n)").rearrange("(z p w) -> z p w", z=2, p=P)[1]
+        parked = parked[:, 0 : POS * PE_TILES * POS].rearrange("p (s w) -> p s w", s=POS)
 
-        def load_x(c):
-            nc.sync.dma_start(out=x_raw[c][:], in_=x_flat[512 * c : 512 * (c + 1), :].rearrange("(j p) c -> p j c", p=P))
+        x_in, e_chan, e_pos, d_img, p_img, p_in, y_rows, y_half, once = {}, {}, {}, {}, {}, {}, {}, {}, {}
+
+        def load_x(c, j0, j1):
+            rows = x_flat[512 * c + P * j0 : 512 * c + P * j1, :]
+            nc.sync.dma_start(out=x_raw[c][:, j0:j1], in_=rows.rearrange("(j p) c -> p j c", p=P))
 
         def load_words(dst, words):
             nc.sync.dma_start(out=dst.bitcast(I32), in_=words.rearrange("p n t -> p (n t)").bitcast(I32))
@@ -89,47 +102,29 @@ def tile_mbconvsqueezeexcitelatestage_x2_kernel(
             for q in range(4):
                 queue.dma_start(out=dst[32 * q : 32 * q + 4].bitcast(I32), in_=rows[4 * q : 4 * q + 4].bitcast(I32))
 
-        nc.vector.memset(w1_raw_plane[:].bitcast(I32), 0)
-        nc.vector.memset(warm[:, 0:1], 0.0)
-        nc.vector.memset(k_pad[:].rearrange("p c a b -> p (c a b)"), 0.0)
-        nc.vector.memset(ws_plane[:].bitcast(I32), 0)
-        nc.vector.memset(w2_plane[:].rearrange("p a f -> p (a f)").bitcast(I32), 0)
-        make_identity(nc, ident[:])
-        nc.scalar.activation(out=warm[:, 1:2], in_=warm[:, 0:1], func=ACT.Silu)
+        def clear(tile):
+            nc.vector.memset(tile[:].rearrange("p r c t s -> p (r c t s)"), 0.0)
 
-        load_x(0)
-        nc.sync.dma_start(
-            out=k_part[:].rearrange("p a (g t) -> p (a g) t", g=2), in_=k_flat.rearrange("a (g p t) -> p (a g) t", g=2, t=4)
-        )
-        load_words(w1_raw[:], w1_words[0])
-        load_scale_rows(nc.sync, w1_raw_plane[:], w1_scales[0])
-        load_x(1)
-        load_x(2)
-        load_x(3)
-        nc.gpsimd.dma_start(out=gs_part[:], in_=gs.rearrange("(p t) -> p t", t=4))
-        load_scale_rows(nc.gpsimd, ws_plane[:], ws_scales[0])
-        nc.gpsimd.dma_start(out=gp_rows[:], in_=gp.partition_broadcast(P))
+        def copy_out(on_scalar, dst, src):
+            if on_scalar:
+                nc.scalar.copy(out=dst, in_=src)
+            else:
+                nc.vector.tensor_copy(out=dst, in_=src)
 
-        nc.vector.tensor_reduce(
-            out=member_f[:], in_=ident[:].rearrange("p (c s) -> p c s", s=POS), axis=AXIS.X, op=ALU.add
-        )
-        for slot in range(2):
-            nc.vector.memset(conv_mat[slot][:].rearrange("p r c t s -> p (r c t s)"), 0.0)
-        nc.vector.tensor_copy(out=member_b[:], in_=member_f[:])
+        def quantize(codes, plane, src):
+            nc.vector.quantize_mx(out=codes.bitcast(FP8X4), scales=plane, in_=src)
 
-        def load_ws():
-            load_words(ws_codes[:], ws_words[0])
-
-        def load_w2():
-            load_scale_rows(nc.sync, w2_plane[:], w2_scales.rearrange("g r n -> r g n"))
-            nc.sync.dma_start(
-                out=w2_codes[:].bitcast(I32), in_=w2_words.rearrange("g p n t -> p g (n t)").bitcast(I32)
+        def mx(out, lhs, lhs_plane, rhs, rhs_plane, start=True, stop=True):
+            nc.tensor.matmul_mx(
+                out=out, lhsT=lhs.bitcast(FP8X4), lhsT_scale=lhs_plane, rhs=rhs.bitcast(FP8X4), rhs_scale=rhs_plane,
+                start=start, stop=stop,
             )
+
 
         def order_w1(tile):
             g, t = divmod(tile, 4)
             for src, dst in ((w1_raw[:].bitcast(I32), w1_codes[:].bitcast(I32)), (w1_raw_plane[:], w1_plane[:])):
-                if tile < 6:
+                if tile < PE_TILES:
                     nc.vector.tensor_copy(
                         out=dst.rearrange("p (g t a c r) -> p g t a c r", g=2, t=4, a=4, c=8)[:, g, t],
                         in_=src.rearrange("p (g a r c t) -> p g t a c r", g=2, t=4, a=4, c=8)[:, g, t],
@@ -140,8 +135,6 @@ def tile_mbconvsqueezeexcitelatestage_x2_kernel(
                         in_=src.rearrange("p (g m t) -> p g t m", g=2, t=4)[:, g, t],
                     )
 
-        x_in = {}
-
         def turn_x(c):
             x_in[c] = placed("x_in", [P, 512 * 4], BF16, 120, bufs=2)
             for h in range(2):
@@ -151,26 +144,11 @@ def tile_mbconvsqueezeexcitelatestage_x2_kernel(
                     for u in range(2):
                         nc.tensor.transpose(ps[:, j, u, :], words[:, u:256:2], ident[:])
                 dst = x_in[c][:].bitcast(F32).rearrange("p (j r u) -> p j r u", j=4, u=2)[:, 2 * h : 2 * h + 2]
-                src = ps[:].rearrange("p j u r -> p j r u")
-                if X_EVAC[2 * c + h] == "v":
-                    nc.vector.tensor_copy(out=dst, in_=src)
-                else:
-                    nc.scalar.copy(out=dst, in_=src)
-
-        def quantize(codes, plane, src):
-            nc.vector.quantize_mx(out=codes.bitcast(FP8X4), scales=plane, in_=src)
+                copy_out(2 * c + h in X_BANKS_ON_SCALAR, dst, ps[:].rearrange("p j u r -> p j r u"))
 
         def quantize_x(c):
             cols = slice(512 * c, 512 * (c + 1))
             quantize(x_codes[:, cols], x_plane[:, cols], x_in[c][:])
-
-        def mx(out, lhs, lhs_plane, rhs, rhs_plane, start=True, stop=True):
-            nc.tensor.matmul_mx(
-                out=out, lhsT=lhs.bitcast(FP8X4), lhsT_scale=lhs_plane, rhs=rhs.bitcast(FP8X4), rhs_scale=rhs_plane,
-                start=start, stop=stop,
-            )
-
-        e_chan = {}
 
         def expand(tile, c):
             ps = bank("mm", [P, 512])
@@ -178,7 +156,7 @@ def tile_mbconvsqueezeexcitelatestage_x2_kernel(
             mx(ps[:], w1_codes[:, ch], w1_plane[:, ch], x_codes[:, cols], x_plane[:, cols])
             pair, side = divmod(tile, 2)
             images = slice(32 * c, 32 * (c + 1))
-            if tile < 6:
+            if tile < PE_TILES:
                 if pair not in e_chan:
                     e_chan[pair] = placed("e_chan%d" % pair, [P, POS, 2, B], F32, 16 * (pair % 2))
                 dst = e_chan[pair][:, :, side, images]
@@ -186,80 +164,36 @@ def tile_mbconvsqueezeexcitelatestage_x2_kernel(
                 dst = e_vec[:, side, :, images]
             nc.scalar.activation(out=dst, in_=ps[:].rearrange("p (b s) -> p s b", s=POS), func=ACT.Silu)
 
-        e_pos = {}
-
-        def regroup(pair, blk):
-            if pair not in e_pos:
-                e_pos[pair] = placed("e_pos%d" % pair, [P, 16, 2, B], F32, 32 + 16 * (pair % 2))
-            for r in range(4):
-                queue = nc.sync if blk == 0 or r == 0 else nc.gpsimd
-                queue.dma_start(
-                    out=e_pos[pair][:, 4 * blk + r].rearrange("p t b -> p (t b)"),
-                    in_=e_chan[pair][32 * blk + r : 32 * blk + 32 : 4].rearrange("p s t b -> p s (t b)"),
-                )
-
-        def build_windows():
-            for tap in range(9):
-                u, v = divmod(tap, 3)
-                nc.scalar.copy(out=k_pad[:, :, 4 - u, 4 - v], in_=k_part[:, tap, 0:6])
-            nc.scalar.copy(out=k_mid[:], in_=k_part[:, 4, 7:8])
-            for pos in range(POS):
-                i, j = divmod(pos, 4)
-                nc.scalar.copy(out=windows[:, pos], in_=k_pad[:, :, 3 - i : 7 - i, 3 - j : 7 - j])
-
-        parked_windows = parked[1].rearrange("p s w -> p (s w)")[:, 0 : POS * 6 * POS].rearrange("p (s w) -> p s w", s=POS)
-
-        def park_windows():
-            nc.sync.dma_start(out=parked_windows, in_=windows[:].rearrange("p s t i j -> p s (t i j)"))
-
-        def fill_conv_mat(pair, queue):
-            by_channel = parked_windows.rearrange("(r c) s w -> c s r w", c=8)
-            for ch in range(8):
-                queue.dma_start(
-                    out=conv_mat[pair % 2][POS * ch : POS * (ch + 1), :, ch].rearrange("p r t s -> p r (t s)"),
-                    in_=by_channel[ch, :, :, 32 * pair : 32 * (pair + 1)],
-                )
-
-        s_in = placed("s_in", [P, B, 4], BF16, 133)
-
-        sums = {}
 
         def squeeze(c):
-            if "ps" not in sums:
-                sums["ps"] = bank("cv", [P, 4, B])
+            if c == 0:
+                once["sums"] = bank("cv", [P, 4, B])
             for j in range(4):
                 images = slice(32 * c + 8 * j, 32 * c + 8 * (j + 1))
                 for t in range(4):
                     nc.tensor.matmul(
-                        sums["ps"][:, t, images], lhsT=x_raw[c][:, j, t:C:4], rhs=member_b[:], start=True, stop=True
+                        once["sums"][:, t, images], lhsT=x_raw[c][:, j, t:C:4], rhs=member_b[:], start=True, stop=True
                     )
 
-        def scale_s():
-            ps = sums["ps"]
+        def quantize_s():
             nc.vector.scalar_tensor_tensor(
-                out=s_in[:], in0=ps[:].rearrange("p t b -> p b t"), scalar=1.0 / POS,
+                out=s_in[:], in0=once["sums"][:].rearrange("p t b -> p b t"), scalar=1.0 / POS,
                 in1=gs_part[:].unsqueeze(1).to_broadcast([P, B, 4]), op0=ALU.mult, op1=ALU.mult,
             )
-
-        def quantize_s():
             quantize(s_codes[:], s_plane[:], s_in[:].rearrange("p b t -> p (b t)"))
 
-        def excite(g):
-            ps = bank("mm", [P, 512])
-            ch = slice(512 * g, 512 * (g + 1))
-            mx(ps[:], s_codes[:], s_plane[:], ws_codes[:, ch], ws_plane[:, ch])
-            nc.scalar.activation(
-                out=gate_img[:, g].rearrange("p m t -> p (m t)"), in_=ps[:], func=ACT.Tanh, scale=0.5
-            )
-
-        def halve_gp():
-            nc.vector.tensor_scalar(out=gp_rows[:], in0=gp_rows[:], scalar1=0.5, scalar2=None, op0=ALU.mult)
-
-        def finish_gate(g):
-            gate = gate_img[:, g].rearrange("p m t -> p (m t)")
-            nc.vector.scalar_tensor_tensor(
-                out=gate, in0=gate, scalar=1.0, in1=gp_rows[:, 512 * g : 512 * (g + 1)], op0=ALU.add, op1=ALU.mult
-            )
+        def excite():
+            gates = [gate_img[:, g].rearrange("p m t -> p (m t)") for g in range(2)]
+            for g in range(2):
+                ps = bank("mm", [P, 512])
+                ch = slice(512 * g, 512 * (g + 1))
+                mx(ps[:], s_codes[:], s_plane[:], ws_codes[:, ch], ws_plane[:, ch])
+                nc.scalar.activation(out=gates[g], in_=ps[:], func=ACT.Tanh, scale=0.5)
+            for g in range(2):
+                nc.vector.scalar_tensor_tensor(
+                    out=gates[g], in0=gates[g], scalar=1.0, in1=gp_rows[:, 512 * g : 512 * (g + 1)],
+                    op0=ALU.add, op1=ALU.mult,
+                )
 
         def turn_gate():
             ps = bank("tr", [P, 2, B])
@@ -267,41 +201,35 @@ def tile_mbconvsqueezeexcitelatestage_x2_kernel(
                 nc.tensor.transpose(ps[:, side, :], gate_img[:, 1, :, 2 + side], ident[:])
             nc.scalar.copy(out=gate_vec[:], in_=ps[:].rearrange("p t b -> p b t"))
 
-        def vec_tap(side, tap, half):
-            u, v = divmod(tap, 3)
-            weight = k_part[:, tap, 6 + side : 7 + side]
-            acc = c_vec[:, side].rearrange("p (i j) b -> p i (j b)", i=4)
-            src = e_vec[:, side].rearrange("p (i j) b -> p i (j b)", i=4)
-            i0, i1 = max(2 * half, 1 - u), min(2 * half + 2, 5 - u)
-            j0, j1 = max(0, 1 - v), min(4, 5 - v)
-            acc = acc[:, i0:i1, B * j0 : B * j1]
-            src = src[:, i0 + u - 1 : i1 + u - 1, B * (j0 + v - 1) : B * (j1 + v - 1)]
-            if tap == 4 and side == 1:
-                nc.scalar.activation(out=acc, in_=src, func=ACT.Copy, scale=k_mid[:])
-            elif tap == 4:
-                nc.vector.tensor_scalar(out=acc, in0=src, scalar1=weight, scalar2=None, op0=ALU.mult)
-            else:
-                nc.vector.scalar_tensor_tensor(out=acc, in0=src, scalar=weight, in1=acc, op0=ALU.mult, op1=ALU.add)
 
-        def vec_silu(side, half):
-            part = c_vec[:, side, 8 * half : 8 * half + 8, :]
-            nc.scalar.activation(out=part, in_=part, func=ACT.Silu)
+        def build_windows():
+            for tap in range(9):
+                u, v = divmod(tap, 3)
+                nc.scalar.copy(out=k_pad[:, :, 4 - u, 4 - v], in_=k_part[:, tap, 0:PE_TILES])
+            nc.scalar.copy(out=k_mid[:], in_=k_part[:, CENTRE, 7:8])
+            for pos in range(POS):
+                i, j = divmod(pos, 4)
+                nc.scalar.copy(out=windows[:, pos], in_=k_pad[:, :, 3 - i : 7 - i, 3 - j : 7 - j])
 
-        halves = {}
+        def fill_conv_mat(pair, queue):
+            by_channel = parked.rearrange("(r c) s w -> c s r w", c=8)
+            for ch in range(8):
+                queue.dma_start(
+                    out=conv_mat[pair % 2][POS * ch : POS * (ch + 1), :, ch].rearrange("p r t s -> p r (t s)"),
+                    in_=by_channel[ch, :, :, 32 * pair : 32 * (pair + 1)],
+                )
 
-        def vec_gate(quarter):
-            if "t" not in halves:
-                halves["t"] = placed("p1_halves", [P, 2, POS, B, 2], BF16, 144)
-            pos = slice(4 * quarter, 4 * quarter + 4)
-            nc.vector.tensor_tensor(
-                out=halves["t"][:, 1, pos], in0=c_vec[:, :, pos, :].rearrange("p t s b -> p s b t"),
-                in1=gate_vec[:].unsqueeze(1).to_broadcast([P, 4, B, 2]), op=ALU.mult,
-            )
-
-        d_img, p_img, p_in = {}, {}, {}
+        def regroup(pair):
+            e_pos[pair] = placed("e_pos%d" % pair, [P, 16, 2, B], F32, 32 + 16 * (pair % 2))
+            for grp in range(16):
+                a, r = divmod(grp, 4)
+                nc.sync.dma_start(
+                    out=e_pos[pair][:, grp].rearrange("p t b -> p (t b)"),
+                    in_=e_chan[pair][32 * a + r : 32 * a + 32 : 4].rearrange("p s t b -> p s (t b)"),
+                )
 
         def convolve(pair, blk, half):
-            if (pair, blk) not in d_img:
+            if half == 0:
                 d_img[pair, blk] = placed("d_img", [P, 2, POS, 32], F32, 120, bufs=6)
             ps = bank("cv", [P, 2, 2, 8, POS])
             for r in range(2):
@@ -331,217 +259,247 @@ def tile_mbconvsqueezeexcitelatestage_x2_kernel(
         def p_words(pair, pos):
             return p_img[pair][:, pos].rearrange("p m t -> p (m t)").bitcast(F32)
 
+
+        def vec_tap(side, tap, half):
+            u, v = divmod(tap, 3)
+            weight = k_part[:, tap, PE_TILES + side : PE_TILES + side + 1]
+            acc = c_vec[:, side].rearrange("p (i j) b -> p i (j b)", i=4)
+            src = e_vec[:, side].rearrange("p (i j) b -> p i (j b)", i=4)
+            i0, i1 = max(2 * half, 1 - u), min(2 * half + 2, 5 - u)
+            j0, j1 = max(0, 1 - v), min(4, 5 - v)
+            acc = acc[:, i0:i1, B * j0 : B * j1]
+            src = src[:, i0 + u - 1 : i1 + u - 1, B * (j0 + v - 1) : B * (j1 + v - 1)]
+            if tap != CENTRE:
+                nc.vector.scalar_tensor_tensor(out=acc, in0=src, scalar=weight, in1=acc, op0=ALU.mult, op1=ALU.add)
+            elif side == 0:
+                nc.vector.tensor_scalar(out=acc, in0=src, scalar1=weight, scalar2=None, op0=ALU.mult)
+            else:
+                nc.scalar.activation(out=acc, in_=src, func=ACT.Copy, scale=k_mid[:])
+
+        def vec_silu(side, half):
+            part = c_vec[:, side, 8 * half : 8 * half + 8, :]
+            nc.scalar.activation(out=part, in_=part, func=ACT.Silu)
+
+        def vec_gate(quarter):
+            if quarter == 0:
+                once["halves"] = placed("p1_halves", [P, 2, POS, B, 2], BF16, 144)
+            pos = slice(4 * quarter, 4 * quarter + 4)
+            nc.vector.tensor_tensor(
+                out=once["halves"][:, 1, pos], in0=c_vec[:, :, pos, :].rearrange("p t s b -> p s b t"),
+                in1=gate_vec[:].unsqueeze(1).to_broadcast([P, 4, B, 2]), op=ALU.mult,
+            )
+
+
+        def new_p_in(g, step):
+            p_in[g, step] = placed("p_in", [P, 2, B, 4], BF16, 54, bufs=4)
+            return p_in[g, step]
+
         def turn_low(step):
             ps = bank("tr", [P, 2, 2, B])
             for s in range(2):
                 for u in range(2):
                     nc.tensor.transpose(ps[:, s, u, :], p_words(u, 2 * step + s), ident[:])
-            p_in[0, step] = placed("p_in", [P, 2, B, 4], BF16, 54, bufs=4)
-            nc.scalar.copy(out=p_in[0, step][:].bitcast(F32), in_=ps[:].rearrange("p s u b -> p s b u"))
+            nc.scalar.copy(out=new_p_in(0, step)[:].bitcast(F32), in_=ps[:].rearrange("p s u b -> p s b u"))
 
-        def quantize_low(step):
-            cols = slice(256 * step, 256 * (step + 1))
-            quantize(p0_codes[:, cols], p0_plane[:, cols], p_in[0, step][:].rearrange("p s b t -> p (s b t)"))
-
-        def turn_high(pos0, pos1):
-            ps = bank("tr", [P, pos1 - pos0, B])
-            for pos in range(pos0, pos1):
-                nc.tensor.transpose(ps[:, pos - pos0, :], p_words(2, pos), ident[:])
-            nc.scalar.copy(
-                out=halves["t"][:, 0, pos0:pos1].rearrange("p s b t -> p s (b t)").bitcast(F32), in_=ps[:]
-            )
+        def turn_high(quarter):
+            ps = bank("tr", [P, 4, B])
+            for s in range(4):
+                nc.tensor.transpose(ps[:, s, :], p_words(2, 4 * quarter + s), ident[:])
+            dst = once["halves"][:, 0, 4 * quarter : 4 * quarter + 4]
+            nc.scalar.copy(out=dst.rearrange("p s b t -> p s (b t)").bitcast(F32), in_=ps[:])
 
         def join_high(step):
-            p_in[1, step] = placed("p_in", [P, 2, B, 4], BF16, 54, bufs=4)
             nc.vector.tensor_copy(
-                out=p_in[1, step][:].rearrange("p s b (h t) -> p (s b) h t", h=2),
-                in_=halves["t"][:, :, 2 * step : 2 * step + 2].rearrange("p h s b t -> p (s b) h t"),
+                out=new_p_in(1, step)[:].rearrange("p s b (h t) -> p (s b) h t", h=2),
+                in_=once["halves"][:, :, 2 * step : 2 * step + 2].rearrange("p h s b t -> p (s b) h t"),
             )
 
-        def quantize_high(step):
+        def quantize_p(g, step):
             cols = slice(256 * step, 256 * (step + 1))
-            quantize(x_codes[:, cols], x_plane[:, cols], p_in[1, step][:].rearrange("p s b t -> p (s b t)"))
+            codes, plane = ((p0_codes, p0_plane), (p1_codes, p1_plane))[g]
+            quantize(codes[:, cols], plane[:, cols], p_in[g, step][:].rearrange("p s b t -> p (s b t)"))
 
-        y_rows, y_half = {}, {}
-        out_rows = out_0.rearrange("b i j n -> b (i j) n")
 
-        def round_y(step, s, src=None):
-            if step not in y_half:
+        def round_y(step, s, src):
+            if s == 0:
                 y_half[step] = placed("y_half", [P, 2, 2, 256], BF16, 48, bufs=3)
-            src = y_rows[step][:, s] if src is None else src
             nc.vector.tensor_copy(
                 out=y_half[step][:, s].rearrange("p u (q e) -> p u q e", e=2),
                 in_=src.rearrange("p (q u e) -> p u q e", u=2, e=2),
             )
 
-        round_inner = round_y
-
         def project(step):
             y_rows[step] = placed("y_rows", [P, 2, N], F32, 80, bufs=4)
             for s in range(2):
-                ps = bank("mm", [P, N])
+                ps = bank("mm" if s == 0 else "cv", [P, N])
                 tok = slice(256 * step + B * s, 256 * step + B * (s + 1))
                 mx(ps[:], p0_codes[:, tok], p0_plane[:, tok], w2_codes[:, 0], w2_plane[:, 0], True, False)
-                mx(ps[:], x_codes[:, tok], x_plane[:, tok], w2_codes[:, 1], w2_plane[:, 1], False, True)
-                if step == 7:
-                    round_inner(step, s, ps[:])
+                mx(ps[:], p1_codes[:, tok], p1_plane[:, tok], w2_codes[:, 1], w2_plane[:, 1], False, True)
+                if step == STEPS - 1:
+                    round_y(step, s, ps[:])
                 nc.scalar.copy(out=y_rows[step][:, s], in_=ps[:])
             nc.sync.dma_start(out=out_rows[:, 2 * step : 2 * step + 2, :], in_=y_rows[step][:])
 
-        y_in = {}
-
         def turn_y(step):
-            if "t" not in y_in:
-                y_in["t"] = placed("y_in", [P, B, POS, 4], BF16, 0)
-            ps = bank("cv", [P, 2, 2, B])
+            if step == 0:
+                once["y_in"] = placed("y_in", [P, B, POS, 4], BF16, 0)
+            ps = bank("tr", [P, 2, 2, B])
             for s in range(2):
                 for u in range(2):
                     nc.tensor.transpose(ps[:, s, u, :], y_half[step][:, s, u, :].bitcast(F32), ident[:])
-            dst = y_in["t"][:].bitcast(F32)[:, :, 2 * step : 2 * step + 2, :]
-            src = ps[:].rearrange("p s u b -> p b s u")
-            if Y_EVAC[step] == "v":
-                nc.vector.tensor_copy(out=dst, in_=src)
-            else:
-                nc.scalar.copy(out=dst, in_=src)
+            dst = once["y_in"][:].bitcast(F32)[:, :, 2 * step : 2 * step + 2, :]
+            copy_out(step in Y_STEPS_ON_SCALAR, dst, ps[:].rearrange("p s u b -> p b s u"))
 
         def store_planes():
             words_out = out_1[0].rearrange("p m t -> p (m t)").bitcast(I32)
-            flat = y_in["t"][:].rearrange("p b s t -> p (b s t)")
-            for c in range(4):
+            flat = once["y_in"][:].rearrange("p b s t -> p (b s t)")
+            for c in range(CHUNKS):
                 cols = slice(512 * c, 512 * (c + 1))
                 quantize(y_codes[:, cols], y_plane[:, cols], flat[:, 2048 * c : 2048 * (c + 1)])
                 nc.sync.dma_start(out=words_out[:, cols], in_=y_codes[:, cols].bitcast(I32))
             for q in range(4):
-                nc.scalar.dma_start(out=out_2[0, 4 * q : 4 * q + 4].bitcast(I32), in_=y_plane[32 * q : 32 * q + 4].bitcast(I32))
+                nc.scalar.dma_start(
+                    out=out_2[0, 4 * q : 4 * q + 4].bitcast(I32), in_=y_plane[32 * q : 32 * q + 4].bitcast(I32)
+                )
 
-        tap_order = (4, 0, 1, 2, 3, 5, 6, 7, 8)
-        taps_left = [(side, tap, half) for side in range(2) for tap in tap_order for half in range(2)]
-        taps_left = [op for op in taps_left if op[:2] != (1, 4)]
 
-        def run_taps(count):
-            for op in [op for op in taps_left if (6 + op[0], 3) not in expands_left][:count]:
-                vec_tap(*op)
-                taps_left.remove(op)
+        nc.vector.memset(w1_raw_plane[:].bitcast(I32), 0)
+        nc.vector.memset(warm[:, 0:1], 0.0)
+        nc.vector.memset(k_pad[:].rearrange("p c a b -> p (c a b)"), 0.0)
+        nc.vector.memset(ws_plane[:].bitcast(I32), 0)
+        nc.vector.memset(w2_plane[:].rearrange("p a f -> p (a f)").bitcast(I32), 0)
+        make_identity(nc, ident[:])
+        nc.scalar.activation(out=warm[:, 1:2], in_=warm[:, 0:1], func=ACT.Silu)
 
+        load_x(0, 0, 2)
+        nc.sync.dma_start(
+            out=k_part[:].rearrange("p a (g t) -> p (a g) t", g=2),
+            in_=k_flat.rearrange("a (g p t) -> p (a g) t", g=2, t=4),
+        )
+        load_x(0, 2, 4)
+        load_x(1, 0, 4)
+        load_words(w1_raw[:], w1_words[0])
+        load_scale_rows(nc.sync, w1_raw_plane[:], w1_scales[0])
+        load_x(2, 0, 4)
+        load_x(3, 0, 4)
+        nc.gpsimd.dma_start(out=gs_part[:], in_=gs.rearrange("(p t) -> p t", t=4))
+        load_scale_rows(nc.gpsimd, ws_plane[:], ws_scales[0])
+        nc.gpsimd.dma_start(out=gp_rows[:], in_=gp.partition_broadcast(P))
+
+        nc.vector.tensor_reduce(
+            out=member_f[:], in_=ident[:].rearrange("p (c s) -> p c s", s=POS), axis=AXIS.X, op=ALU.add
+        )
+        clear(conv_mat[0])
+        nc.vector.tensor_copy(out=member_b[:], in_=member_f[:])
         build_windows()
-        load_ws()
-        park_windows()
+        load_words(ws_codes[:], ws_words[0])
+        nc.sync.dma_start(out=parked, in_=windows[:].rearrange("p s t i j -> p s (t i j)"))
         fill_conv_mat(0, nc.sync)
-        fill_conv_mat(1, nc.gpsimd)
-        order_w1(0)
-        order_w1(1)
+
         turn_x(0)
         quantize_x(0)
         turn_x(1)
-        for c in range(4):
-            if c < 3:
+        order_w1(0)
+        order_w1(1)
+        next_tiles = (6, 2, 3, 7)
+        for c in range(CHUNKS):
+            if c + 1 < CHUNKS:
                 quantize_x(c + 1)
-            if c < 2:
+            if c + 2 < CHUNKS:
                 turn_x(c + 2)
             expand(0, c)
             expand(1, c)
-            if c < 3:
+            if c + 1 < CHUNKS:
                 squeeze(c)
-            order_w1((6, 2, 3, 7)[c])
-        for blk in range(4):
-            regroup(0, blk)
+            order_w1(next_tiles[c])
+        regroup(0)
         order_w1(4)
         order_w1(5)
-        halve_gp()
-        tile_order = ((6,), (7,), (2, 3), (4, 5))
-        expands_left = [(tile, c) for group in tile_order for c in range(4) for tile in group]
+        nc.vector.tensor_scalar(out=gp_rows[:], in0=gp_rows[:], scalar1=0.5, scalar2=None, op0=ALU.mult)
+        clear(conv_mat[1])
+        fill_conv_mat(1, nc.gpsimd)
+
+        expands_left = [(tile, c) for tiles in ((6,), (2, 3), (7,), (4, 5)) for c in range(CHUNKS) for tile in tiles]
+        tap_order = (CENTRE, 0, 1, 2, 3, 5, 6, 7, 8)
+        taps_left = [(side, tap, half) for side in range(2) for tap in tap_order for half in range(2)]
+        taps_left = [op for op in taps_left if op[:2] != (1, CENTRE)]
+        last = CHUNKS - 1
 
         def run_expands(count):
             for tile, c in expands_left[:count]:
                 expand(tile, c)
                 expands_left.remove((tile, c))
-                if (tile, c) == (3, 3):
-                    for blk in range(4):
-                        regroup(1, blk)
-                if (tile, c) == (7, 3):
-                    vec_tap(1, 4, 0)
-                    vec_tap(1, 4, 1)
+                if (tile, c) == (3, last):
+                    regroup(1)
+                if (tile, c) == (7, last):
+                    vec_tap(1, CENTRE, 0)
+                    vec_tap(1, CENTRE, 1)
 
-        for c in range(3, 4):
-            run_expands(1)
-            squeeze(c)
-        run_taps(1)
-        scale_s()
-        run_taps(0)
+        def run_taps(count):
+            ready = [op for op in taps_left if (PE_TILES + op[0], last) not in expands_left]
+            for op in ready[:count]:
+                vec_tap(*op)
+                taps_left.remove(op)
+
+        run_expands(1)
+        squeeze(last)
         quantize_s()
-        run_expands(6)
-        if -1 < 0:
-            excite(0)
-            excite(1)
-        run_taps(4)
-        if -1 < 0:
-            finish_gate(0)
-            finish_gate(1)
-        run_expands(0)
-        run_taps(8)
-        blocks_left = [(pair, blk) for pair in range(3) for blk in range(4)][:11]
-        rounds = [(pair, blk, side) for pair in range(3) for blk in range(4) for side in range(2)]
-        for n, (pair, blk, side) in enumerate(rounds):
-            convolve(pair, blk, side)
-            run_expands(2)
-            if n == -1:
-                excite(0)
-                excite(1)
-                finish_gate(0)
-                finish_gate(1)
-            if n == 1:
+        run_expands(8)
+        run_taps(14)
+
+        rounds = [(pair, blk, half) for pair in range(3) for blk in range(4) for half in range(2)]
+        for n, (pair, blk, half) in enumerate(rounds):
+            convolve(pair, blk, half)
+            if half == 1:
+                run_expands(3)
+            if n == 0:
+                excite()
+            if (pair, blk, half) == (0, 3, 0):
                 turn_gate()
-            if n == 7:
-                fill_conv_mat(2, nc.sync)
-            if n == 8:
-                for late in range(4):
-                    regroup(2, late)
-                load_w2()
-            if side == 1:
-                for done in blocks_left[: 1 if n < 10 else 2]:
-                    if 8 * done[0] + 2 * done[1] + 2 * (1 if n < 10 else 0) < n:
-                        gate_block(*done)
-                        blocks_left.remove(done)
+            if (pair, blk, half) == (0, 3, 1):
+                fill_conv_mat(2, nc.gpsimd)
+            if (pair, blk, half) == (1, 2, 0):
+                regroup(2)
+                load_scale_rows(nc.sync, w2_plane[:], w2_scales.rearrange("g r n -> r g n"))
+                nc.sync.dma_start(
+                    out=w2_codes[:].bitcast(I32), in_=w2_words.rearrange("g p n t -> p g (n t)").bitcast(I32)
+                )
+            if half == 1:
+                if n < len(rounds) - 1:
+                    gate_block(pair, blk)
                 run_taps(3)
-            if n in (13, 13 + 1):
-                vec_silu(0, n - 13)
-            if n in (16, 16 + 1):
-                vec_silu(1, n - 16)
-            if n >= 17 and side == 1:
-                first = 2 * ((n - 17) // 2)
-                for step in range(first, min(first + 2, 8)):
-                    turn_low(step)
-            if n >= 17 + 2 and side == 1:
-                first = 2 * ((n - 17) // 2 - 1)
-                for step in range(first, min(first + 2, 8)):
-                    quantize_low(step)
-            if n >= 16 and side == 0 and (n - 16) // 2 < 4:
-                vec_gate((n - 16) // 2)
+            if (pair, blk) == (1, 2):
+                vec_silu(0, half)
+            if (pair, blk) == (2, 0):
+                vec_silu(1, half)
+            if pair == 2 and half == 1:
+                turn_low(2 * blk)
+                turn_low(2 * blk + 1)
+                if blk > 0:
+                    quantize_p(0, 2 * blk - 2)
+                    quantize_p(0, 2 * blk - 1)
+            if pair == 2 and half == 0:
+                vec_gate(blk)
+
         for quarter in range(4):
             gate_block(2, 3, 4 * quarter, 4 * quarter + 4)
-        done_low = min(8, 2 * ((23 - 17) // 2 + 1))
-        done_q = min(8, 2 * ((23 - 17) // 2))
-        for step in range(done_low, 8):
-            turn_low(step)
-        done_gate = min(4, (22 - 16) // 2 + 1)
-        for it in range(8 + 5):
-            if it < 4:
-                turn_high(4 * it, 4 * it + 4)
-            if it % 1 == 0:
-                for step in range(it - 5, it - 5 + 1):
-                    if 0 <= step < 8:
-                        turn_y(step)
-            if done_gate + it < 4:
-                vec_gate(done_gate + it)
-            if it < 8:
+
+        run = BANKS["tr"]
+        for it in range(STEPS + 2 * run):
+            if it % run == 0:
+                for quarter in range(it, min(it + run, 4)):
+                    turn_high(quarter)
+                for step in range(max(it - 2 * run, 0), min(it - run, STEPS)):
+                    turn_y(step)
+            if it < STEPS:
                 join_high(it)
-            if done_q + it < 8:
-                quantize_low(done_q + it)
-            if 3 <= it < 7 + 3:
-                round_y(it - 3, 0)
-                round_y(it - 3, 1)
-            if it < 8:
-                quantize_high(it)
-            if 2 <= it < 8 + 2:
+            if it < 2:
+                quantize_p(0, STEPS - 2 + it)
+            if 3 <= it < STEPS + 2:
+                for s in range(2):
+                    round_y(it - 3, s, y_rows[it - 3][:, s])
+            if it < STEPS:
+                quantize_p(1, it)
+            if 2 <= it < STEPS + 2:
                 project(it - 2)
         store_planes()

from contextlib import ExitStack

import concourse.mybir as mybir
from concourse.masks import make_identity

F32 = mybir.dt.float32
BF16 = mybir.dt.bfloat16
I32 = mybir.dt.int32
U32 = mybir.dt.uint32
U8 = mybir.dt.uint8
FP8X4 = mybir.dt.float8_e4m3fn_x4
ALU = mybir.AluOpType
ACT = mybir.ActivationFunctionType
AXIS = mybir.AxisListType

P = 128
B, POS, C, F, N = 128, 16, 512, 1024, 512
TOK = B * POS
FLOPS = 2 * TOK * C * F + 2 * B * C * F + 2 * TOK * F * N + 2 * 9 * TOK * F
KIB = 1024

CHUNKS = 4
PE_TILES = 6
STEPS = 8
CENTRE = 4
BANKS = {"mm": 3, "tr": 3, "cv": 2}
X_BANKS_ON_SCALAR = (2, 4, 6)
Y_STEPS_ON_SCALAR = (0, 2, 4)


def tile_mbconvsqueezeexcitelatestage_x2_kernel(
    tc, x, w1_words, w1_scales, k, gs, ws_words, ws_scales, gp, w2_words, w2_scales, out_0, out_1, out_2
):
    nc = tc.nc
    with ExitStack() as ctx:
        big = ctx.enter_context(tc.tile_pool(name="big", bufs=1))
        keep = ctx.enter_context(tc.tile_pool(name="keep", bufs=1))
        psum = ctx.enter_context(tc.psum_pool(name="psum", bufs=1))
        ctx.enter_context(tc.manual_schedule())

        def placed(name, shape, dtype, kib, bufs=1):
            return big.tile(shape, dtype, name=name, tag=name, bufs=bufs, align_bytes=64, offset=kib * KIB)

        def kept(name, shape, dtype):
            return keep.tile(shape, dtype, name=name, tag=name, align_bytes=64)

        def bank(role, shape):
            return psum.tile(shape, F32, name=role, tag=role, bufs=BANKS[role])

        ident = kept("ident", [P, P], F32)
        member_f = kept("member_f", [P, 8], F32)
        member_b = kept("member_b", [P, 8], BF16)
        warm = kept("warm", [P, 2], F32)
        k_part = kept("k_part", [P, 9, 8], BF16)
        k_mid = kept("k_mid", [P, 1], F32)
        gs_part = kept("gs_part", [P, 4], BF16)
        w2_plane = kept("w2_plane", [P, 2, N], U8)
        w2_codes = kept("w2_codes", [P, 2, N], U32)
        w1_codes = kept("w1_codes", [P, F], U32)
        w1_plane = kept("w1_plane", [P, F], U8)
        ws_codes = kept("ws_codes", [P, F], U32)
        ws_plane = kept("ws_plane", [P, F], U8)
        x_codes = kept("x_codes", [P, TOK], U32)
        x_plane = kept("x_plane", [P, TOK], U8)
        s_codes = kept("s_codes", [P, B], U32)
        s_plane = kept("s_plane", [P, B], U8)
        p0_codes = kept("p0_codes", [P, TOK], U32)
        p0_plane = kept("p0_plane", [P, TOK], U8)
        p1_codes, p1_plane = x_codes, x_plane
        y_codes = kept("y_codes", [P, TOK], U32)
        y_plane = kept("y_plane", [P, TOK], U8)
        gate_img = kept("gate_img", [P, 2, P, 4], F32)
        gate_vec = kept("gate_vec", [P, B, 2], F32)

        x_raw = [placed("x_raw%d" % c, [P, 4, C], BF16, 96 + 4 * c) for c in range(CHUNKS)]
        gp_rows = placed("gp_rows", [P, F], BF16, 136)
        windows = placed("windows", [P, POS, PE_TILES, 4, 4], F32, 112)
        k_pad = placed("k_pad", [P, PE_TILES, 7, 8], F32, 118)
        w1_raw = placed("w1_raw", [P, F], U32, 128)
        w1_raw_plane = placed("w1_raw_plane", [P, F], U8, 132)
        conv_mat = [placed("conv_mat%d" % slot, [P, 16, 8, 2, POS], F32, 64 + 16 * slot) for slot in range(2)]
        e_vec = placed("e_vec", [P, 2, POS, B], F32, 144)
        c_vec = placed("c_vec", [P, 2, POS, B], F32, 160)
        s_in = placed("s_in", [P, B, 4], BF16, 133)

        x_flat = x.rearrange("b i j c -> (b i j) c")
        k_flat = k.rearrange("u v f -> (u v) f")
        out_rows = out_0.rearrange("b i j n -> b (i j) n")
        parked = out_0.rearrange("b i j n -> (b i j n)").rearrange("(z p w) -> z p w", z=2, p=P)[1]
        parked = parked[:, 0 : POS * PE_TILES * POS].rearrange("p (s w) -> p s w", s=POS)

        x_in, e_chan, e_pos, d_img, p_img, p_in, y_rows, y_half, once = {}, {}, {}, {}, {}, {}, {}, {}, {}

        def load_x(c, j0, j1):
            rows = x_flat[512 * c + P * j0 : 512 * c + P * j1, :]
            nc.sync.dma_start(out=x_raw[c][:, j0:j1], in_=rows.rearrange("(j p) c -> p j c", p=P))

        def load_words(dst, words):
            nc.sync.dma_start(out=dst.bitcast(I32), in_=words.rearrange("p n t -> p (n t)").bitcast(I32))

        def load_scale_rows(queue, dst, rows):
            for q in range(4):
                queue.dma_start(out=dst[32 * q : 32 * q + 4].bitcast(I32), in_=rows[4 * q : 4 * q + 4].bitcast(I32))

        def clear(tile):
            nc.vector.memset(tile[:].rearrange("p r c t s -> p (r c t s)"), 0.0)

        def copy_out(on_scalar, dst, src):
            if on_scalar:
                nc.scalar.copy(out=dst, in_=src)
            else:
                nc.vector.tensor_copy(out=dst, in_=src)

        def quantize(codes, plane, src):
            nc.vector.quantize_mx(out=codes.bitcast(FP8X4), scales=plane, in_=src)

        def mx(out, lhs, lhs_plane, rhs, rhs_plane, start=True, stop=True):
            nc.tensor.matmul_mx(
                out=out, lhsT=lhs.bitcast(FP8X4), lhsT_scale=lhs_plane, rhs=rhs.bitcast(FP8X4), rhs_scale=rhs_plane,
                start=start, stop=stop,
            )


        def order_w1(tile):
            g, t = divmod(tile, 4)
            for src, dst in ((w1_raw[:].bitcast(I32), w1_codes[:].bitcast(I32)), (w1_raw_plane[:], w1_plane[:])):
                if tile < PE_TILES:
                    nc.vector.tensor_copy(
                        out=dst.rearrange("p (g t a c r) -> p g t a c r", g=2, t=4, a=4, c=8)[:, g, t],
                        in_=src.rearrange("p (g a r c t) -> p g t a c r", g=2, t=4, a=4, c=8)[:, g, t],
                    )
                else:
                    nc.vector.tensor_copy(
                        out=dst.rearrange("p (g t m) -> p g t m", g=2, t=4)[:, g, t],
                        in_=src.rearrange("p (g m t) -> p g t m", g=2, t=4)[:, g, t],
                    )

        def turn_x(c):
            x_in[c] = placed("x_in", [P, 512 * 4], BF16, 120, bufs=2)
            for h in range(2):
                ps = bank("tr", [P, 2, 2, P])
                for j in range(2):
                    words = x_raw[c][:, 2 * h + j, :].bitcast(F32)
                    for u in range(2):
                        nc.tensor.transpose(ps[:, j, u, :], words[:, u:256:2], ident[:])
                dst = x_in[c][:].bitcast(F32).rearrange("p (j r u) -> p j r u", j=4, u=2)[:, 2 * h : 2 * h + 2]
                copy_out(2 * c + h in X_BANKS_ON_SCALAR, dst, ps[:].rearrange("p j u r -> p j r u"))

        def quantize_x(c):
            cols = slice(512 * c, 512 * (c + 1))
            quantize(x_codes[:, cols], x_plane[:, cols], x_in[c][:])

        def expand(tile, c):
            ps = bank("mm", [P, 512])
            ch, cols = slice(P * tile, P * (tile + 1)), slice(512 * c, 512 * (c + 1))
            mx(ps[:], w1_codes[:, ch], w1_plane[:, ch], x_codes[:, cols], x_plane[:, cols])
            pair, side = divmod(tile, 2)
            images = slice(32 * c, 32 * (c + 1))
            if tile < PE_TILES:
                if pair not in e_chan:
                    e_chan[pair] = placed("e_chan%d" % pair, [P, POS, 2, B], F32, 16 * (pair % 2))
                dst = e_chan[pair][:, :, side, images]
            else:
                dst = e_vec[:, side, :, images]
            nc.scalar.activation(out=dst, in_=ps[:].rearrange("p (b s) -> p s b", s=POS), func=ACT.Silu)


        def squeeze(c):
            if c == 0:
                once["sums"] = bank("cv", [P, 4, B])
            for j in range(4):
                images = slice(32 * c + 8 * j, 32 * c + 8 * (j + 1))
                for t in range(4):
                    nc.tensor.matmul(
                        once["sums"][:, t, images], lhsT=x_raw[c][:, j, t:C:4], rhs=member_b[:], start=True, stop=True
                    )

        def quantize_s():
            nc.vector.scalar_tensor_tensor(
                out=s_in[:], in0=once["sums"][:].rearrange("p t b -> p b t"), scalar=1.0 / POS,
                in1=gs_part[:].unsqueeze(1).to_broadcast([P, B, 4]), op0=ALU.mult, op1=ALU.mult,
            )
            quantize(s_codes[:], s_plane[:], s_in[:].rearrange("p b t -> p (b t)"))

        def excite():
            gates = [gate_img[:, g].rearrange("p m t -> p (m t)") for g in range(2)]
            for g in range(2):
                ps = bank("mm", [P, 512])
                ch = slice(512 * g, 512 * (g + 1))
                mx(ps[:], s_codes[:], s_plane[:], ws_codes[:, ch], ws_plane[:, ch])
                nc.scalar.activation(out=gates[g], in_=ps[:], func=ACT.Tanh, scale=0.5)
            for g in range(2):
                nc.vector.scalar_tensor_tensor(
                    out=gates[g], in0=gates[g], scalar=1.0, in1=gp_rows[:, 512 * g : 512 * (g + 1)],
                    op0=ALU.add, op1=ALU.mult,
                )

        def turn_gate():
            ps = bank("tr", [P, 2, B])
            for side in range(2):
                nc.tensor.transpose(ps[:, side, :], gate_img[:, 1, :, 2 + side], ident[:])
            nc.scalar.copy(out=gate_vec[:], in_=ps[:].rearrange("p t b -> p b t"))


        def build_windows():
            for tap in range(9):
                u, v = divmod(tap, 3)
                nc.scalar.copy(out=k_pad[:, :, 4 - u, 4 - v], in_=k_part[:, tap, 0:PE_TILES])
            nc.scalar.copy(out=k_mid[:], in_=k_part[:, CENTRE, 7:8])
            for pos in range(POS):
                i, j = divmod(pos, 4)
                nc.scalar.copy(out=windows[:, pos], in_=k_pad[:, :, 3 - i : 7 - i, 3 - j : 7 - j])

        def fill_conv_mat(pair, queue):
            by_channel = parked.rearrange("(r c) s w -> c s r w", c=8)
            for ch in range(8):
                queue.dma_start(
                    out=conv_mat[pair % 2][POS * ch : POS * (ch + 1), :, ch].rearrange("p r t s -> p r (t s)"),
                    in_=by_channel[ch, :, :, 32 * pair : 32 * (pair + 1)],
                )

        def regroup(pair):
            e_pos[pair] = placed("e_pos%d" % pair, [P, 16, 2, B], F32, 32 + 16 * (pair % 2))
            for grp in range(16):
                a, r = divmod(grp, 4)
                nc.sync.dma_start(
                    out=e_pos[pair][:, grp].rearrange("p t b -> p (t b)"),
                    in_=e_chan[pair][32 * a + r : 32 * a + 32 : 4].rearrange("p s t b -> p s (t b)"),
                )

        def convolve(pair, blk, half):
            if half == 0:
                d_img[pair, blk] = placed("d_img", [P, 2, POS, 32], F32, 120, bufs=6)
            ps = bank("cv", [P, 2, 2, 8, POS])
            for r in range(2):
                grp = 4 * blk + 2 * half + r
                for side in range(2):
                    nc.tensor.matmul(
                        ps[:, side, r], lhsT=e_pos[pair][:, grp, side, :], rhs=conv_mat[pair % 2][:, grp, :, side, :],
                        start=True, stop=True,
                    )
            nc.scalar.activation(
                out=d_img[pair, blk][:, :, :, 16 * half : 16 * (half + 1)],
                in_=ps[:].rearrange("p t r c s -> p t s (r c)"), func=ACT.Silu,
            )

        def gate_block(pair, blk, pos0=0, pos1=POS):
            if pair not in p_img:
                p_img[pair] = placed("p_img%d" % pair, [P, POS, P, 2], BF16, 96 + 8 * pair)
            g, u = divmod(pair, 2)
            ch = slice(32 * blk, 32 * (blk + 1))
            nc.vector.tensor_tensor(
                out=p_img[pair][:, pos0:pos1, ch, :],
                in0=d_img[pair, blk][:, :, pos0:pos1, :].rearrange("p t s m -> p s m t"),
                in1=gate_img[:, g, ch, 2 * u : 2 * u + 2].unsqueeze(1).to_broadcast([P, pos1 - pos0, 32, 2]),
                op=ALU.mult,
            )

        def p_words(pair, pos):
            return p_img[pair][:, pos].rearrange("p m t -> p (m t)").bitcast(F32)


        def vec_tap(side, tap, half):
            u, v = divmod(tap, 3)
            weight = k_part[:, tap, PE_TILES + side : PE_TILES + side + 1]
            acc = c_vec[:, side].rearrange("p (i j) b -> p i (j b)", i=4)
            src = e_vec[:, side].rearrange("p (i j) b -> p i (j b)", i=4)
            i0, i1 = max(2 * half, 1 - u), min(2 * half + 2, 5 - u)
            j0, j1 = max(0, 1 - v), min(4, 5 - v)
            acc = acc[:, i0:i1, B * j0 : B * j1]
            src = src[:, i0 + u - 1 : i1 + u - 1, B * (j0 + v - 1) : B * (j1 + v - 1)]
            if tap != CENTRE:
                nc.vector.scalar_tensor_tensor(out=acc, in0=src, scalar=weight, in1=acc, op0=ALU.mult, op1=ALU.add)
            elif side == 0:
                nc.vector.tensor_scalar(out=acc, in0=src, scalar1=weight, scalar2=None, op0=ALU.mult)
            else:
                nc.scalar.activation(out=acc, in_=src, func=ACT.Copy, scale=k_mid[:])

        def vec_silu(side, half):
            part = c_vec[:, side, 8 * half : 8 * half + 8, :]
            nc.scalar.activation(out=part, in_=part, func=ACT.Silu)

        def vec_gate(quarter):
            if quarter == 0:
                once["halves"] = placed("p1_halves", [P, 2, POS, B, 2], BF16, 144)
            pos = slice(4 * quarter, 4 * quarter + 4)
            nc.vector.tensor_tensor(
                out=once["halves"][:, 1, pos], in0=c_vec[:, :, pos, :].rearrange("p t s b -> p s b t"),
                in1=gate_vec[:].unsqueeze(1).to_broadcast([P, 4, B, 2]), op=ALU.mult,
            )


        def new_p_in(g, step):
            p_in[g, step] = placed("p_in", [P, 2, B, 4], BF16, 54, bufs=4)
            return p_in[g, step]

        def turn_low(step):
            ps = bank("tr", [P, 2, 2, B])
            for s in range(2):
                for u in range(2):
                    nc.tensor.transpose(ps[:, s, u, :], p_words(u, 2 * step + s), ident[:])
            nc.scalar.copy(out=new_p_in(0, step)[:].bitcast(F32), in_=ps[:].rearrange("p s u b -> p s b u"))

        def turn_high(quarter):
            ps = bank("tr", [P, 4, B])
            for s in range(4):
                nc.tensor.transpose(ps[:, s, :], p_words(2, 4 * quarter + s), ident[:])
            dst = once["halves"][:, 0, 4 * quarter : 4 * quarter + 4]
            nc.scalar.copy(out=dst.rearrange("p s b t -> p s (b t)").bitcast(F32), in_=ps[:])

        def join_high(step):
            nc.vector.tensor_copy(
                out=new_p_in(1, step)[:].rearrange("p s b (h t) -> p (s b) h t", h=2),
                in_=once["halves"][:, :, 2 * step : 2 * step + 2].rearrange("p h s b t -> p (s b) h t"),
            )

        def quantize_p(g, step):
            cols = slice(256 * step, 256 * (step + 1))
            codes, plane = ((p0_codes, p0_plane), (p1_codes, p1_plane))[g]
            quantize(codes[:, cols], plane[:, cols], p_in[g, step][:].rearrange("p s b t -> p (s b t)"))


        def round_y(step, s, src):
            if s == 0:
                y_half[step] = placed("y_half", [P, 2, 2, 256], BF16, 48, bufs=3)
            nc.vector.tensor_copy(
                out=y_half[step][:, s].rearrange("p u (q e) -> p u q e", e=2),
                in_=src.rearrange("p (q u e) -> p u q e", u=2, e=2),
            )

        def project(step):
            y_rows[step] = placed("y_rows", [P, 2, N], F32, 80, bufs=4)
            for s in range(2):
                ps = bank("mm" if s == 0 else "cv", [P, N])
                tok = slice(256 * step + B * s, 256 * step + B * (s + 1))
                mx(ps[:], p0_codes[:, tok], p0_plane[:, tok], w2_codes[:, 0], w2_plane[:, 0], True, False)
                mx(ps[:], p1_codes[:, tok], p1_plane[:, tok], w2_codes[:, 1], w2_plane[:, 1], False, True)
                if step == STEPS - 1:
                    round_y(step, s, ps[:])
                nc.scalar.copy(out=y_rows[step][:, s], in_=ps[:])
            nc.sync.dma_start(out=out_rows[:, 2 * step : 2 * step + 2, :], in_=y_rows[step][:])

        def turn_y(step):
            if step == 0:
                once["y_in"] = placed("y_in", [P, B, POS, 4], BF16, 0)
            ps = bank("tr", [P, 2, 2, B])
            for s in range(2):
                for u in range(2):
                    nc.tensor.transpose(ps[:, s, u, :], y_half[step][:, s, u, :].bitcast(F32), ident[:])
            dst = once["y_in"][:].bitcast(F32)[:, :, 2 * step : 2 * step + 2, :]
            copy_out(step in Y_STEPS_ON_SCALAR, dst, ps[:].rearrange("p s u b -> p b s u"))

        def store_planes():
            words_out = out_1[0].rearrange("p m t -> p (m t)").bitcast(I32)
            flat = once["y_in"][:].rearrange("p b s t -> p (b s t)")
            for c in range(CHUNKS):
                cols = slice(512 * c, 512 * (c + 1))
                quantize(y_codes[:, cols], y_plane[:, cols], flat[:, 2048 * c : 2048 * (c + 1)])
                nc.sync.dma_start(out=words_out[:, cols], in_=y_codes[:, cols].bitcast(I32))
            for q in range(4):
                nc.scalar.dma_start(
                    out=out_2[0, 4 * q : 4 * q + 4].bitcast(I32), in_=y_plane[32 * q : 32 * q + 4].bitcast(I32)
                )


        nc.vector.memset(w1_raw_plane[:].bitcast(I32), 0)
        nc.vector.memset(warm[:, 0:1], 0.0)
        nc.vector.memset(k_pad[:].rearrange("p c a b -> p (c a b)"), 0.0)
        nc.vector.memset(ws_plane[:].bitcast(I32), 0)
        nc.vector.memset(w2_plane[:].rearrange("p a f -> p (a f)").bitcast(I32), 0)
        make_identity(nc, ident[:])
        nc.scalar.activation(out=warm[:, 1:2], in_=warm[:, 0:1], func=ACT.Silu)

        load_x(0, 0, 2)
        nc.sync.dma_start(
            out=k_part[:].rearrange("p a (g t) -> p (a g) t", g=2),
            in_=k_flat.rearrange("a (g p t) -> p (a g) t", g=2, t=4),
        )
        load_x(0, 2, 4)
        load_x(1, 0, 4)
        load_words(w1_raw[:], w1_words[0])
        load_scale_rows(nc.sync, w1_raw_plane[:], w1_scales[0])
        load_x(2, 0, 4)
        load_x(3, 0, 4)
        nc.gpsimd.dma_start(out=gs_part[:], in_=gs.rearrange("(p t) -> p t", t=4))
        load_scale_rows(nc.gpsimd, ws_plane[:], ws_scales[0])
        nc.gpsimd.dma_start(out=gp_rows[:], in_=gp.partition_broadcast(P))

        nc.vector.tensor_reduce(
            out=member_f[:], in_=ident[:].rearrange("p (c s) -> p c s", s=POS), axis=AXIS.X, op=ALU.add
        )
        clear(conv_mat[0])
        nc.vector.tensor_copy(out=member_b[:], in_=member_f[:])
        build_windows()
        load_words(ws_codes[:], ws_words[0])
        nc.sync.dma_start(out=parked, in_=windows[:].rearrange("p s t i j -> p s (t i j)"))
        fill_conv_mat(0, nc.sync)

        turn_x(0)
        quantize_x(0)
        turn_x(1)
        order_w1(0)
        order_w1(1)
        next_tiles = (6, 2, 3, 7)
        for c in range(CHUNKS):
            if c + 1 < CHUNKS:
                quantize_x(c + 1)
            if c + 2 < CHUNKS:
                turn_x(c + 2)
            expand(0, c)
            expand(1, c)
            if c + 1 < CHUNKS:
                squeeze(c)
            order_w1(next_tiles[c])
        regroup(0)
        order_w1(4)
        order_w1(5)
        nc.vector.tensor_scalar(out=gp_rows[:], in0=gp_rows[:], scalar1=0.5, scalar2=None, op0=ALU.mult)
        clear(conv_mat[1])
        fill_conv_mat(1, nc.gpsimd)

        expands_left = [(tile, c) for tiles in ((6,), (2, 3), (7,), (4, 5)) for c in range(CHUNKS) for tile in tiles]
        tap_order = (CENTRE, 0, 1, 2, 3, 5, 6, 7, 8)
        taps_left = [(side, tap, half) for side in range(2) for tap in tap_order for half in range(2)]
        taps_left = [op for op in taps_left if op[:2] != (1, CENTRE)]
        last = CHUNKS - 1

        def run_expands(count):
            for tile, c in expands_left[:count]:
                expand(tile, c)
                expands_left.remove((tile, c))
                if (tile, c) == (3, last):
                    regroup(1)
                if (tile, c) == (7, last):
                    vec_tap(1, CENTRE, 0)
                    vec_tap(1, CENTRE, 1)

        def run_taps(count):
            ready = [op for op in taps_left if (PE_TILES + op[0], last) not in expands_left]
            for op in ready[:count]:
                vec_tap(*op)
                taps_left.remove(op)

        run_expands(1)
        squeeze(last)
        quantize_s()
        run_expands(8)
        run_taps(14)

        rounds = [(pair, blk, half) for pair in range(3) for blk in range(4) for half in range(2)]
        for n, (pair, blk, half) in enumerate(rounds):
            convolve(pair, blk, half)
            if half == 1:
                run_expands(3)
            if n == 0:
                excite()
            if (pair, blk, half) == (0, 3, 0):
                turn_gate()
            if (pair, blk, half) == (0, 3, 1):
                fill_conv_mat(2, nc.gpsimd)
            if (pair, blk, half) == (1, 2, 0):
                regroup(2)
                load_scale_rows(nc.sync, w2_plane[:], w2_scales.rearrange("g r n -> r g n"))
                nc.sync.dma_start(
                    out=w2_codes[:].bitcast(I32), in_=w2_words.rearrange("g p n t -> p g (n t)").bitcast(I32)
                )
            if half == 1:
                if n < len(rounds) - 1:
                    gate_block(pair, blk)
                run_taps(3)
            if (pair, blk) == (1, 2):
                vec_silu(0, half)
            if (pair, blk) == (2, 0):
                vec_silu(1, half)
            if pair == 2 and half == 1:
                turn_low(2 * blk)
                turn_low(2 * blk + 1)
                if blk > 0:
                    quantize_p(0, 2 * blk - 2)
                    quantize_p(0, 2 * blk - 1)
            if pair == 2 and half == 0:
                vec_gate(blk)

        for quarter in range(4):
            gate_block(2, 3, 4 * quarter, 4 * quarter + 4)

        run = BANKS["tr"]
        for it in range(STEPS + 2 * run):
            if it % run == 0:
                for quarter in range(it, min(it + run, 4)):
                    turn_high(quarter)
                for step in range(max(it - 2 * run, 0), min(it - run, STEPS)):
                    turn_y(step)
            if it < STEPS:
                join_high(it)
            if it < 2:
                quantize_p(0, STEPS - 2 + it)
            if 3 <= it < STEPS + 2:
                for s in range(2):
                    round_y(it - 3, s, y_rows[it - 3][:, s])
            if it < STEPS:
                quantize_p(1, it)
            if 2 <= it < STEPS + 2:
                project(it - 2)
        store_planes()
